import numpy as np
import ml_dtypes


def mxq(x, axis, fmt="e4m3"):
    dtype, down = {"e4m3": (ml_dtypes.float8_e4m3fn, 7), "e5m2": (ml_dtypes.float8_e5m2, 14)}[fmt]
    v = np.moveaxis(np.asarray(x, np.float32).astype(ml_dtypes.bfloat16).astype(np.float64), axis, -1)
    blocks = v.reshape(v.shape[:-1] + (-1, 32))
    amax = np.abs(blocks).max(-1, keepdims=True)
    byte = np.maximum(np.where(amax > 0, np.frexp(amax)[1] - 1 + 127, 0) - down, 1)
    scale = np.exp2(byte - 127.0)
    codes = (blocks / scale).astype(np.float32).astype(dtype).astype(np.float64)
    return np.moveaxis((codes * scale).reshape(v.shape), -1, axis)


WIDE = False


def mx_kscale(k):
    if not WIDE:
        return np.ones(k)
    levels = np.array([30, -30])
    if k % 512:
        return np.exp2(np.random.permutation(np.resize(levels, k // 32))).repeat(32)
    a = np.empty((k // 512, 16))
    for p in range(k // 512):
        a[p, :8] = np.random.permutation(np.resize(levels, 8))
        for g in range(8):
            far = levels[np.abs(levels - a[p, g]) >= 10]
            a[p, g + 8] = far[np.random.randint(len(far))]
    return np.exp2(a.ravel()).repeat(32)


BF16 = ml_dtypes.bfloat16


def bf(x):
    return np.asarray(x, np.float32).astype(BF16)


def f64(x):
    return np.asarray(x).astype(np.float64)


T, C, D, N, L, J = 2048, 1024, 512, 1024, 24, 1


def setup_inputs():
    s = mx_kscale(C)
    t = mx_kscale(D)
    x = np.random.standard_normal((T + L, C)) * s
    e = np.random.standard_t(5.0, (D, T + J)) * t[:, None]
    return {"x": bf(x),
            "e": bf(e),
            "a": bf(0.5 + 0.1 * np.random.standard_normal(C)),
            "c": bf(0.6 + 0.1 * np.random.standard_normal(D)),
            "w": bf(np.random.standard_normal((C, N)) / np.sqrt(C) / s[:, None]),
            "v": bf(np.random.standard_normal((D, N)) / np.sqrt(D) / t[:, None]),
            "bias": bf(0.3 * np.random.standard_normal(N))}


def reference(x, e, a, c, w, v, bias):
    x, e = f64(x), f64(e)
    m = x[L:] + f64(a) * x[:T]
    r = e[:, J:] + f64(c)[:, None] * e[:, :T]
    y_m = mxq(m, 1, "e4m3") @ mxq(f64(w), 0, "e4m3")
    y_r = mxq(r, 0, "e5m2").T @ mxq(f64(v), 0, "e4m3")
    return y_m + y_r + f64(bias)

@@ -1,0 +1,415 @@
+from contextlib import ExitStack
+
+import concourse.mybir as mybir
+from concourse.masks import make_identity
+
+T, C, D, N, LAG = 2048, 1024, 512, 1024, 24
+FLOPS = 2 * T * (C + D) * N
+
+F32 = mybir.dt.float32
+BF16 = mybir.dt.bfloat16
+U32 = mybir.dt.uint32
+U8 = mybir.dt.uint8
+E4 = mybir.dt.float8_e4m3fn_x4
+E5 = mybir.dt.float8_e5m2_x4
+COPY = mybir.ActivationFunctionType.Copy
+ADD = mybir.AluOpType.add
+MULT = mybir.AluOpType.mult
+
+P = 128
+GROUP = 256
+GROUPS = T // GROUP
+HALF = 512
+ECH = 512
+EROW = 528
+RUN = 8
+
+ORDER = [
+    ("Lx", 0,),
+    ("Lw", 0, 0,),
+    ("Le", 0,),
+    ("Lx", 1,),
+    ("Lw", 1, 0,),
+    ("Lw", 2, 0,),
+    ("Lx", 2,),
+    ("Lw", 0, 1,),
+    ("Lw", 1, 1,),
+    ("Lx", 3,),
+    ("Le", 1,),
+    ("Lw", 2, 1,),
+    ("Lx", 4,),
+    ("Lx", 5,),
+    ("Le", 2,),
+    ("Lx", 6,),
+    ("Le", 3,),
+    ("Lx", 7,),
+    ("B", "V",),
+    ("H", "V",),
+    ("T", 0,),
+    ("A", 0, 0,),
+    ("A", 0, 1,),
+    ("I", 0, 0, "V",),
+    ("T", 1,),
+    ("Qw", 0, 0,),
+    ("C", 0, "G",),
+    ("R", 0, "G",),
+    ("M", 0, 0,),
+    ("M", 0, 1,),
+    ("A", 1, 0,),
+    ("A", 1, 1,),
+    ("M", 1, 0,),
+    ("M", 1, 1,),
+    ("I", 2, 0, "S",),
+    ("T", 2,),
+    ("A", 2, 0,),
+    ("A", 2, 1,),
+    ("T", 3,),
+    ("C", 1, "G",),
+    ("Qm", 0,),
+    ("I", 1, 0, "V",),
+    ("Qm", 1,),
+    ("Qw", 1, 0,),
+    ("Qw", 2, 0,),
+    ("Qr", 0,),
+    ("X", 0, 0, 0,),
+    ("X", 0, 1, 0,),
+    ("R", 1, "G",),
+    ("C", 2, "G",),
+    ("I", 0, 1, "S",),
+    ("M", 2, 0,),
+    ("E", 0, 0, 0,),
+    ("S", 0, 0, 0,),
+    ("M", 2, 1,),
+    ("A", 3, 0,),
+    ("A", 3, 1,),
+    ("T", 4,),
+    ("E", 0, 1, 0,),
+    ("S", 0, 1, 0,),
+    ("Qm", 2,),
+    ("Qw", 0, 1,),
+    ("Qr", 1,),
+    ("X", 1, 0, 0,),
+    ("X", 1, 1, 0,),
+    ("R", 2, "G",),
+    ("C", 3, "G",),
+    ("I", 1, 1, "S",),
+    ("M", 3, 0,),
+    ("E", 1, 0, 0,),
+    ("S", 1, 0, 0,),
+    ("M", 3, 1,),
+    ("A", 4, 0,),
+    ("A", 4, 1,),
+    ("T", 5,),
+    ("E", 1, 1, 0,),
+    ("S", 1, 1, 0,),
+    ("Qm", 3,),
+    ("Qw", 1, 1,),
+    ("Qr", 2,),
+    ("X", 2, 0, 0,),
+    ("X", 2, 1, 0,),
+    ("R", 3, "G",),
+    ("C", 4, "G",),
+    ("I", 2, 1, "S",),
+    ("M", 4, 0,),
+    ("E", 2, 0, 0,),
+    ("S", 2, 0, 0,),
+    ("M", 4, 1,),
+    ("A", 5, 0,),
+    ("A", 5, 1,),
+    ("T", 6,),
+    ("E", 2, 1, 0,),
+    ("S", 2, 1, 0,),
+    ("Qm", 4,),
+    ("Qw", 2, 1,),
+    ("Qr", 3,),
+    ("X", 0, 0, 1,),
+    ("X", 0, 1, 1,),
+    ("X", 1, 0, 1,),
+    ("X", 1, 1, 1,),
+    ("R", 4, "G",),
+    ("C", 5, "S",),
+    ("C", 6, "S",),
+    ("M", 5, 0,),
+    ("E", 0, 0, 1,),
+    ("S", 0, 0, 1,),
+    ("X", 3, 0, 0,),
+    ("M", 5, 1,),
+    ("A", 6, 0,),
+    ("A", 6, 1,),
+    ("T", 7,),
+    ("Qm", 5,),
+    ("Qr", 4,),
+    ("R", 5, "G",),
+    ("E", 0, 1, 1,),
+    ("S", 0, 1, 1,),
+    ("X", 3, 1, 0,),
+    ("E", 1, 0, 1,),
+    ("S", 1, 0, 1,),
+    ("X", 2, 0, 1,),
+    ("E", 1, 1, 1,),
+    ("S", 1, 1, 1,),
+    ("X", 2, 1, 1,),
+    ("E", 3, 0, 0,),
+    ("S", 3, 0, 0,),
+    ("E", 3, 1, 0,),
+    ("S", 3, 1, 0,),
+    ("E", 2, 0, 1,),
+    ("S", 2, 0, 1,),
+    ("E", 2, 1, 1,),
+    ("S", 2, 1, 1,),
+    ("Qr", 5,),
+    ("X", 3, 0, 1,),
+    ("X", 3, 1, 1,),
+    ("X", 4, 0, 0,),
+    ("X", 4, 1, 0,),
+    ("R", 6, "G",),
+    ("C", 7, "S",),
+    ("M", 6, 0,),
+    ("E", 3, 0, 1,),
+    ("S", 3, 0, 1,),
+    ("X", 4, 0, 1,),
+    ("M", 6, 1,),
+    ("A", 7, 0,),
+    ("A", 7, 1,),
+    ("E", 3, 1, 1,),
+    ("S", 3, 1, 1,),
+    ("X", 4, 1, 1,),
+    ("E", 4, 0, 0,),
+    ("S", 4, 0, 0,),
+    ("X", 5, 0, 0,),
+    ("E", 4, 1, 0,),
+    ("S", 4, 1, 0,),
+    ("X", 5, 1, 0,),
+    ("E", 4, 0, 1,),
+    ("S", 4, 0, 1,),
+    ("E", 4, 1, 1,),
+    ("S", 4, 1, 1,),
+    ("Qm", 6,),
+    ("Qr", 6,),
+    ("E", 5, 0, 0,),
+    ("S", 5, 0, 0,),
+    ("E", 5, 1, 0,),
+    ("S", 5, 1, 0,),
+    ("X", 5, 0, 1,),
+    ("X", 5, 1, 1,),
+    ("X", 6, 0, 0,),
+    ("X", 6, 1, 0,),
+    ("R", 7, "G",),
+    ("M", 7, 0,),
+    ("E", 5, 0, 1,),
+    ("S", 5, 0, 1,),
+    ("X", 6, 0, 1,),
+    ("M", 7, 1,),
+    ("E", 5, 1, 1,),
+    ("S", 5, 1, 1,),
+    ("X", 6, 1, 1,),
+    ("E", 6, 0, 0,),
+    ("S", 6, 0, 0,),
+    ("E", 6, 1, 0,),
+    ("S", 6, 1, 0,),
+    ("Qm", 7,),
+    ("Qr", 7,),
+    ("E", 6, 0, 1,),
+    ("S", 6, 0, 1,),
+    ("E", 6, 1, 1,),
+    ("S", 6, 1, 1,),
+    ("X", 7, 0, 0,),
+    ("X", 7, 1, 0,),
+    ("X", 7, 0, 1,),
+    ("X", 7, 1, 1,),
+    ("E", 7, 0, 0,),
+    ("S", 7, 0, 0,),
+    ("E", 7, 1, 0,),
+    ("S", 7, 1, 0,),
+    ("E", 7, 0, 1,),
+    ("S", 7, 0, 1,),
+    ("E", 7, 1, 1,),
+    ("S", 7, 1, 1,),
+]
+
+
+def tile_lag_channel_mix_s2_kernel(tc, x, e, a, c, w, v, bias, out):
+    nc = tc.nc
+    with ExitStack() as ctx:
+        keep = ctx.enter_context(tc.tile_pool(name="keep", bufs=1))
+        work = ctx.enter_context(tc.tile_pool(name="work", bufs=2))
+        psum = ctx.enter_context(tc.psum_pool(name="psum", bufs=2))
+        ctx.enter_context(tc.manual_schedule())
+        eng = {"V": nc.vector, "S": nc.scalar, "G": nc.gpsimd, "SP": nc.sync}
+
+        ident = keep.tile([P, P], F32, name="ident")
+        hist = keep.tile([P, C], BF16, name="hist")
+        a_bf = keep.tile([P, 2, 4], BF16, name="a_bf")
+        c_bf = keep.tile([P, 4], BF16, name="c_bf")
+        b_bf = keep.tile([P, 8], BF16, name="b_bf")
+        a32 = keep.tile([P, 8], F32, name="a32")
+        c32 = keep.tile([P, 4], F32, name="c32")
+        bias_bc = keep.tile([P, N], BF16, name="bias_bc")
+        ax = [keep.tile([P, T // RUN, 4, RUN], F32, name="ax%d" % g) for g in range(2)]
+        xs = [keep.tile([P, 2, C], BF16, name="x%d" % i) for i in range(GROUPS)]
+        es = [keep.tile([P, 4, EROW], BF16, name="e%d" % i) for i in range(T // ECH)]
+        wraw, wcodes, wscales = {}, {}, {}
+        for g in range(3):
+            for h in range(2):
+                wraw[g, h] = keep.tile([P, 4, HALF], BF16, name="wraw%d%d" % (g, h))
+                wcodes[g, h] = keep.tile([P, HALF], U32, name="wcodes%d%d" % (g, h), align_bytes=64)
+                wscales[g, h] = keep.tile([P, HALF], U8, name="wscales%d%d" % (g, h), align_bytes=64)
+        mcodes = [keep.tile([P, 2 * GROUP], U32, name="mcodes%d" % i, align_bytes=64) for i in range(GROUPS)]
+        mscales = [keep.tile([P, 2 * GROUP], U8, name="mscales%d" % i, align_bytes=64) for i in range(GROUPS)]
+        rcodes = [keep.tile([P, GROUP], U32, name="rcodes%d" % i, align_bytes=64) for i in range(GROUPS)]
+        rscales = [keep.tile([P, GROUP], U8, name="rscales%d" % i, align_bytes=64) for i in range(GROUPS)]
+        live = {}
+
+        nc.vector.memset(hist[:], 0.0)
+        make_identity(nc, ident[:])
+        nc.scalar.dma_start(out=a_bf[:], in_=a.rearrange("(g p t) -> p g t", g=2, t=4))
+        nc.scalar.dma_start(out=b_bf[:], in_=bias.rearrange("(p j) -> p j", j=8))
+        nc.scalar.dma_start(out=c_bf[:], in_=c.rearrange("(p t) -> p t", t=4))
+        nc.scalar.dma_start(out=hist[0:LAG, :], in_=x[0:LAG, :])
+        nc.scalar.activation(out=a32[:], in_=a_bf[:].rearrange("p g t -> p (g t)"), func=COPY)
+        nc.scalar.activation(out=c32[:], in_=c_bf[:], func=COPY)
+
+        def copy(engine, dst, src):
+            if engine == "S":
+                nc.scalar.copy(out=dst, in_=src)
+            else:
+                eng[engine].tensor_copy(out=dst, in_=src)
+
+        def scale(engine, dst, src, factor):
+            if engine == "S":
+                nc.scalar.activation(out=dst, in_=src, func=COPY, scale=factor)
+            else:
+                eng[engine].tensor_scalar(out=dst, in0=src, scalar1=factor, scalar2=0.0, op0=MULT, op1=ADD)
+
+        def load_x(i):
+            rows = x[LAG + GROUP * i : LAG + GROUP * (i + 1), :]
+            nc.sync.dma_start(out=xs[i][:], in_=rows.rearrange("(s p) c -> p s c", p=P))
+
+        def load_e(i):
+            src = e.rearrange("(p j) t -> p j t", j=4)
+            nc.sync.dma_start(out=es[i][:, :, 0 : ECH + 1], in_=src[:, :, ECH * i : ECH * (i + 1) + 1])
+
+        def load_w(g, h):
+            rows = w[512 * g : 512 * (g + 1), :] if g < 2 else v
+            src = rows.rearrange("(p j) n -> p j n", j=4)
+            nc.sync.dma_start(out=wraw[g, h][:], in_=src[:, :, HALF * h : HALF * (h + 1)])
+
+        def spread_bias(engine):
+            bank = psum.tile([P, 4, P], F32, name="bias_bank", tag="acc", bufs=4)
+            words = b_bf[:].bitcast(F32)
+            for j in range(4):
+                nc.tensor.transpose(bank[:, j, :], words[:, j : j + 1].to_broadcast([P, P]), ident[:])
+            dst = bias_bc[:].bitcast(F32).rearrange("p (n j) -> p n j", j=4)
+            copy(engine, dst, bank[:].rearrange("p j n -> p n j"))
+
+        def history(engine):
+            bank = psum.tile([P, 4, P], F32, name="hist_bank", tag="acc", bufs=4)
+            words = hist[:].bitcast(F32)
+            for g in range(2):
+                for u in range(2):
+                    nc.tensor.transpose(bank[:, 2 * g + u, :], words[:, 256 * g + u : 256 * (g + 1) : 2], ident[:])
+            halves = bank[:].rearrange("p q r -> p (q r)").bitcast(BF16)
+            halves = halves.rearrange("p (q b t e) -> p q e b t", q=4, t=RUN, e=2)
+            for g in range(2):
+                for s in range(4):
+                    scale(engine, ax[g][:, 0 : LAG // RUN, s, :], halves[:, 2 * g + s // 2, s % 2, 0 : LAG // RUN, :],
+                          a32[:, 4 * g + s : 4 * g + s + 1])
+
+        def turn(i):
+            for g in range(2):
+                bank = psum.tile([P, 2, GROUP], F32, name="xt%d" % g, tag="xt%d" % g, bufs=2)
+                live["xt", i, g] = bank
+                for s in range(2):
+                    words = xs[i][:, s, :].bitcast(F32)
+                    for u in range(2):
+                        nc.tensor.transpose(bank[:, u, P * s : P * (s + 1)], words[:, 256 * g + u : 256 * (g + 1) : 2], ident[:])
+
+        def lagged(i, g):
+            halves = live["xt", i, g][:].rearrange("p u r -> p (u r)").bitcast(BF16)
+            halves = halves.rearrange("p (u b t e) -> p u e b t", u=2, t=RUN, e=2)
+            first = (LAG + GROUP * i) // RUN
+            count = min(GROUP // RUN, T // RUN - first)
+            for s in range(4):
+                scale("S", ax[g][:, first : first + count, s, :], halves[:, s // 2, s % 2, 0:count, :],
+                      a32[:, 4 * g + s : 4 * g + s + 1])
+
+        def mix_m(i, g):
+            if g == 0:
+                live["m", i] = work.tile([P, 2, 4 * GROUP], BF16, name="m_il", align_bytes=64, bufs=2)
+            halves = live["xt", i, g][:].rearrange("p u r -> p (u r)").bitcast(BF16)
+            first = GROUP * i // RUN
+            nc.vector.tensor_tensor(
+                out=live["m", i][:, g, :].rearrange("p (b t u e) -> p b t u e", t=RUN, u=2, e=2),
+                in0=halves.rearrange("p (u b t e) -> p b t u e", u=2, t=RUN, e=2),
+                in1=ax[g][:, first : first + GROUP // RUN, :, :].rearrange("p b (u e) t -> p b t u e", e=2),
+                op=ADD,
+            )
+
+        def quant_m(i):
+            nc.vector.quantize_mx(out=mcodes[i][:].bitcast(E4), scales=mscales[i][:],
+                                  in_=live["m", i][:].rearrange("p g k -> p (g k)"))
+
+        def scale_e(i, engine):
+            live["ce", i] = work.tile([P, 4, GROUP], F32, name="ce")
+            off = GROUP * (i % 2)
+            for j in range(4):
+                scale(engine, live["ce", i][:, j, :], es[i // 2][:, j, off : off + GROUP], c32[:, j : j + 1])
+
+        def mix_r(i, engine):
+            live["r", i] = work.tile([P, 4 * GROUP], BF16, name="r_il", align_bytes=64, bufs=1)
+            off = GROUP * (i % 2) + 1
+            eng[engine].tensor_tensor(
+                out=live["r", i][:].rearrange("p (t j) -> p t j", j=4),
+                in0=es[i // 2][:, :, off : off + GROUP].rearrange("p j t -> p t j"),
+                in1=live["ce", i][:].rearrange("p j t -> p t j"),
+                op=ADD,
+            )
+
+        def quant_r(i):
+            nc.vector.quantize_mx(out=rcodes[i][:].bitcast(E5), scales=rscales[i][:], in_=live["r", i][:])
+
+        def weave_w(g, h, engine):
+            live["w", g, h] = work.tile([P, HALF, 4], BF16, name="w_il", align_bytes=64, bufs=3)
+            copy(engine, live["w", g, h][:].rearrange("p (c i) t -> p c t i", i=4),
+                 wraw[g, h][:].rearrange("p t (c i) -> p c t i", i=4))
+
+        def quant_w(g, h):
+            nc.vector.quantize_mx(out=wcodes[g, h][:].bitcast(E4), scales=wscales[g, h][:],
+                                  in_=live["w", g, h][:].rearrange("p n t -> p (n t)"))
+
+        def multiply(i, s, h):
+            acc = psum.tile([P, HALF], F32, name="acc", tag="acc", bufs=4)
+            live["acc", i, s, h] = acc
+            for g in range(2):
+                cols = slice(GROUP * g + P * s, GROUP * g + P * (s + 1))
+                nc.tensor.matmul_mx(out=acc[:], lhsT=mcodes[i][:, cols].bitcast(E4), lhsT_scale=mscales[i][:, cols],
+                                    rhs=wcodes[g, h][:].bitcast(E4), rhs_scale=wscales[g, h][:],
+                                    start=(g == 0), stop=False)
+            cols = slice(P * s, P * (s + 1))
+            nc.tensor.matmul_mx(out=acc[:], lhsT=rcodes[i][:, cols].bitcast(E5), lhsT_scale=rscales[i][:, cols],
+                                rhs=wcodes[2, h][:].bitcast(E4), rhs_scale=wscales[2, h][:],
+                                start=False, stop=True)
+
+        def finish(i, s, h):
+            y = work.tile([P, HALF], F32, name="y", bufs=8)
+            live["y", i, s, h] = y
+            nc.vector.tensor_tensor(out=y[:], in0=live["acc", i, s, h][:], in1=bias_bc[:, HALF * h : HALF * (h + 1)], op=ADD)
+
+        def empty(i, s, h):
+            y = work.tile([P, HALF], F32, name="y", bufs=8)
+            live["y", i, s, h] = y
+            nc.scalar.copy(out=y[:], in_=live["acc", i, s, h][:])
+
+        def add_bias(i, s, h):
+            y = live["y", i, s, h]
+            nc.gpsimd.tensor_tensor(out=y[:], in0=y[:], in1=bias_bc[:, HALF * h : HALF * (h + 1)], op=ADD)
+
+        def store(i, s, h):
+            row = GROUP * i + P * s
+            nc.sync.dma_start(out=out[row : row + P, HALF * h : HALF * (h + 1)], in_=live["y", i, s, h][:])
+
+        steps = {"Lx": load_x, "Le": load_e, "Lw": load_w, "B": spread_bias, "H": history, "T": turn, "A": lagged,
+                 "M": mix_m, "Qm": quant_m, "C": scale_e, "R": mix_r, "Qr": quant_r, "I": weave_w, "Qw": quant_w,
+                 "X": multiply, "E": finish, "F": empty, "Gb": add_bias, "S": store}
+        for step in ORDER:
+            steps[step[0]](*step[1:])

@@ -12,7 +12,6 @@ U32 = mybir.dt.uint32
 U8 = mybir.dt.uint8
 E4 = mybir.dt.float8_e4m3fn_x4
 E5 = mybir.dt.float8_e5m2_x4
-COPY = mybir.ActivationFunctionType.Copy
 ADD = mybir.AluOpType.add
 MULT = mybir.AluOpType.mult
 
@@ -22,187 +21,202 @@ GROUPS = T // GROUP
 HALF = 512
 ECH = 512
 EROW = 528
-RUN = 8
 
 ORDER = [
-    ("Lx", 0,),
-    ("Lw", 0, 0,),
     ("Le", 0,),
-    ("Lx", 1,),
+    ("Lw", 0, 0,),
     ("Lw", 1, 0,),
+    ("Lx", 0,),
     ("Lw", 2, 0,),
-    ("Lx", 2,),
-    ("Lw", 0, 1,),
-    ("Lw", 1, 1,),
-    ("Lx", 3,),
     ("Le", 1,),
+    ("Lw", 0, 1,),
+    ("Lx", 1,),
+    ("Lw", 1, 1,),
     ("Lw", 2, 1,),
+    ("Le", 2,),
+    ("Lx", 2,),
+    ("Le", 3,),
+    ("Lx", 3,),
     ("Lx", 4,),
     ("Lx", 5,),
-    ("Le", 2,),
     ("Lx", 6,),
-    ("Le", 3,),
     ("Lx", 7,),
-    ("B", "V",),
-    ("H", "V",),
+    ("B", "S",),
+    ("H", "S",),
+    ("R", 0, "V",),
+    ("R", 1, "V",),
+    ("I", 0, 0, "S",),
+    ("I", 1, 0, "V",),
+    ("JR", 0, "S",),
     ("T", 0,),
-    ("A", 0, 0,),
-    ("A", 0, 1,),
-    ("I", 0, 0, "V",),
-    ("T", 1,),
+    ("K", 0, 0,),
+    ("K", 0, 1,),
     ("Qw", 0, 0,),
-    ("C", 0, "G",),
-    ("R", 0, "G",),
+    ("Qw", 1, 0,),
+    ("Qr", 0,),
     ("M", 0, 0,),
     ("M", 0, 1,),
-    ("A", 1, 0,),
-    ("A", 1, 1,),
+    ("I", 2, 0, "S",),
+    ("R", 2, "V",),
+    ("R", 3, "V",),
+    ("Qw", 2, 0,),
+    ("T", 1,),
+    ("J", 0, 0, "S",),
+    ("J", 0, 1, "S",),
+    ("K", 1, 0,),
+    ("K", 1, 1,),
+    ("I", 0, 1, "V",),
+    ("I", 1, 1, "S",),
+    ("Qm", 0,),
     ("M", 1, 0,),
     ("M", 1, 1,),
-    ("I", 2, 0, "S",),
     ("T", 2,),
-    ("A", 2, 0,),
-    ("A", 2, 1,),
+    ("Qw", 0, 1,),
+    ("I", 2, 1, "S",),
+    ("R", 4, "V",),
+    ("K", 2, 0,),
+    ("K", 2, 1,),
+    ("Qw", 1, 1,),
+    ("R", 5, "V",),
+    ("Qw", 2, 1,),
     ("T", 3,),
-    ("C", 1, "G",),
-    ("Qm", 0,),
-    ("I", 1, 0, "V",),
-    ("Qm", 1,),
-    ("Qw", 1, 0,),
-    ("Qw", 2, 0,),
-    ("Qr", 0,),
     ("X", 0, 0, 0,),
     ("X", 0, 1, 0,),
-    ("R", 1, "G",),
-    ("C", 2, "G",),
-    ("I", 0, 1, "S",),
+    ("X", 0, 0, 1,),
+    ("X", 0, 1, 1,),
+    ("J", 1, 0, "S",),
+    ("J", 1, 1, "S",),
+    ("JR", 1, "S",),
+    ("K", 3, 0,),
+    ("K", 3, 1,),
     ("M", 2, 0,),
     ("E", 0, 0, 0,),
     ("S", 0, 0, 0,),
     ("M", 2, 1,),
-    ("A", 3, 0,),
-    ("A", 3, 1,),
-    ("T", 4,),
     ("E", 0, 1, 0,),
     ("S", 0, 1, 0,),
-    ("Qm", 2,),
-    ("Qw", 0, 1,),
+    ("Qm", 1,),
     ("Qr", 1,),
+    ("T", 4,),
+    ("E", 0, 0, 1,),
+    ("S", 0, 0, 1,),
+    ("E", 0, 1, 1,),
+    ("S", 0, 1, 1,),
     ("X", 1, 0, 0,),
     ("X", 1, 1, 0,),
-    ("R", 2, "G",),
-    ("C", 3, "G",),
-    ("I", 1, 1, "S",),
+    ("X", 1, 0, 1,),
+    ("X", 1, 1, 1,),
+    ("J", 2, 0, "S",),
+    ("J", 2, 1, "S",),
+    ("JR", 2, "S",),
+    ("K", 4, 0,),
+    ("K", 4, 1,),
     ("M", 3, 0,),
     ("E", 1, 0, 0,),
     ("S", 1, 0, 0,),
     ("M", 3, 1,),
-    ("A", 4, 0,),
-    ("A", 4, 1,),
-    ("T", 5,),
     ("E", 1, 1, 0,),
     ("S", 1, 1, 0,),
-    ("Qm", 3,),
-    ("Qw", 1, 1,),
+    ("Qm", 2,),
     ("Qr", 2,),
+    ("T", 5,),
+    ("E", 1, 0, 1,),
+    ("S", 1, 0, 1,),
+    ("E", 1, 1, 1,),
+    ("S", 1, 1, 1,),
     ("X", 2, 0, 0,),
     ("X", 2, 1, 0,),
-    ("R", 3, "G",),
-    ("C", 4, "G",),
-    ("I", 2, 1, "S",),
+    ("X", 2, 0, 1,),
+    ("X", 2, 1, 1,),
+    ("J", 3, 0, "S",),
+    ("J", 3, 1, "S",),
+    ("JR", 3, "S",),
+    ("K", 5, 0,),
+    ("K", 5, 1,),
     ("M", 4, 0,),
     ("E", 2, 0, 0,),
     ("S", 2, 0, 0,),
     ("M", 4, 1,),
-    ("A", 5, 0,),
-    ("A", 5, 1,),
-    ("T", 6,),
+    ("R", 6, "V",),
     ("E", 2, 1, 0,),
     ("S", 2, 1, 0,),
-    ("Qm", 4,),
-    ("Qw", 2, 1,),
+    ("Qm", 3,),
     ("Qr", 3,),
-    ("X", 0, 0, 1,),
-    ("X", 0, 1, 1,),
-    ("X", 1, 0, 1,),
-    ("X", 1, 1, 1,),
-    ("R", 4, "G",),
-    ("C", 5, "S",),
-    ("C", 6, "S",),
-    ("M", 5, 0,),
-    ("E", 0, 0, 1,),
-    ("S", 0, 0, 1,),
-    ("X", 3, 0, 0,),
-    ("M", 5, 1,),
-    ("A", 6, 0,),
-    ("A", 6, 1,),
-    ("T", 7,),
-    ("Qm", 5,),
-    ("Qr", 4,),
-    ("R", 5, "G",),
-    ("E", 0, 1, 1,),
-    ("S", 0, 1, 1,),
-    ("X", 3, 1, 0,),
-    ("E", 1, 0, 1,),
-    ("S", 1, 0, 1,),
-    ("X", 2, 0, 1,),
-    ("E", 1, 1, 1,),
-    ("S", 1, 1, 1,),
-    ("X", 2, 1, 1,),
-    ("E", 3, 0, 0,),
-    ("S", 3, 0, 0,),
-    ("E", 3, 1, 0,),
-    ("S", 3, 1, 0,),
+    ("T", 6,),
     ("E", 2, 0, 1,),
     ("S", 2, 0, 1,),
     ("E", 2, 1, 1,),
     ("S", 2, 1, 1,),
-    ("Qr", 5,),
+    ("X", 3, 0, 0,),
+    ("X", 3, 1, 0,),
     ("X", 3, 0, 1,),
     ("X", 3, 1, 1,),
-    ("X", 4, 0, 0,),
-    ("X", 4, 1, 0,),
-    ("R", 6, "G",),
-    ("C", 7, "S",),
-    ("M", 6, 0,),
+    ("J", 4, 0, "S",),
+    ("J", 4, 1, "S",),
+    ("JR", 4, "S",),
+    ("K", 6, 0,),
+    ("K", 6, 1,),
+    ("M", 5, 0,),
+    ("E", 3, 0, 0,),
+    ("S", 3, 0, 0,),
+    ("M", 5, 1,),
+    ("R", 7, "V",),
+    ("E", 3, 1, 0,),
+    ("S", 3, 1, 0,),
+    ("Qm", 4,),
+    ("Qr", 4,),
+    ("T", 7,),
     ("E", 3, 0, 1,),
     ("S", 3, 0, 1,),
-    ("X", 4, 0, 1,),
-    ("M", 6, 1,),
-    ("A", 7, 0,),
-    ("A", 7, 1,),
     ("E", 3, 1, 1,),
     ("S", 3, 1, 1,),
+    ("X", 4, 0, 0,),
+    ("X", 4, 1, 0,),
+    ("X", 4, 0, 1,),
     ("X", 4, 1, 1,),
+    ("J", 5, 0, "S",),
+    ("J", 5, 1, "S",),
+    ("JR", 5, "S",),
+    ("K", 7, 0,),
+    ("K", 7, 1,),
+    ("M", 6, 0,),
     ("E", 4, 0, 0,),
     ("S", 4, 0, 0,),
-    ("X", 5, 0, 0,),
+    ("M", 6, 1,),
     ("E", 4, 1, 0,),
     ("S", 4, 1, 0,),
-    ("X", 5, 1, 0,),
+    ("Qm", 5,),
+    ("Qr", 5,),
     ("E", 4, 0, 1,),
     ("S", 4, 0, 1,),
     ("E", 4, 1, 1,),
     ("S", 4, 1, 1,),
-    ("Qm", 6,),
-    ("Qr", 6,),
-    ("E", 5, 0, 0,),
-    ("S", 5, 0, 0,),
-    ("E", 5, 1, 0,),
-    ("S", 5, 1, 0,),
+    ("X", 5, 0, 0,),
+    ("X", 5, 1, 0,),
     ("X", 5, 0, 1,),
     ("X", 5, 1, 1,),
-    ("X", 6, 0, 0,),
-    ("X", 6, 1, 0,),
-    ("R", 7, "G",),
+    ("J", 6, 0, "S",),
+    ("J", 6, 1, "S",),
+    ("JR", 6, "S",),
     ("M", 7, 0,),
+    ("E", 5, 0, 0,),
+    ("S", 5, 0, 0,),
+    ("M", 7, 1,),
+    ("E", 5, 1, 0,),
+    ("S", 5, 1, 0,),
+    ("Qm", 6,),
+    ("Qr", 6,),
     ("E", 5, 0, 1,),
     ("S", 5, 0, 1,),
-    ("X", 6, 0, 1,),
-    ("M", 7, 1,),
     ("E", 5, 1, 1,),
     ("S", 5, 1, 1,),
+    ("X", 6, 0, 0,),
+    ("X", 6, 1, 0,),
+    ("X", 6, 0, 1,),
     ("X", 6, 1, 1,),
+    ("J", 7, 0, "S",),
+    ("J", 7, 1, "S",),
+    ("JR", 7, "S",),
     ("E", 6, 0, 0,),
     ("S", 6, 0, 0,),
     ("E", 6, 1, 0,),
@@ -242,10 +256,8 @@ def tile_lag_channel_mix_s2_kernel(tc, x, e, a, c, w, v, bias, out):
         a_bf = keep.tile([P, 2, 4], BF16, name="a_bf")
         c_bf = keep.tile([P, 4], BF16, name="c_bf")
         b_bf = keep.tile([P, 8], BF16, name="b_bf")
-        a32 = keep.tile([P, 8], F32, name="a32")
-        c32 = keep.tile([P, 4], F32, name="c32")
         bias_bc = keep.tile([P, N], BF16, name="bias_bc")
-        ax = [keep.tile([P, T // RUN, 4, RUN], F32, name="ax%d" % g) for g in range(2)]
+        xw = [keep.tile([P, T], F32, name="xw%d" % q) for q in range(4)]
         xs = [keep.tile([P, 2, C], BF16, name="x%d" % i) for i in range(GROUPS)]
         es = [keep.tile([P, 4, EROW], BF16, name="e%d" % i) for i in range(T // ECH)]
         wraw, wcodes, wscales = {}, {}, {}
@@ -266,20 +278,12 @@ def tile_lag_channel_mix_s2_kernel(tc, x, e, a, c, w, v, bias, out):
         nc.scalar.dma_start(out=b_bf[:], in_=bias.rearrange("(p j) -> p j", j=8))
         nc.scalar.dma_start(out=c_bf[:], in_=c.rearrange("(p t) -> p t", t=4))
         nc.scalar.dma_start(out=hist[0:LAG, :], in_=x[0:LAG, :])
-        nc.scalar.activation(out=a32[:], in_=a_bf[:].rearrange("p g t -> p (g t)"), func=COPY)
-        nc.scalar.activation(out=c32[:], in_=c_bf[:], func=COPY)
 
         def copy(engine, dst, src):
             if engine == "S":
                 nc.scalar.copy(out=dst, in_=src)
             else:
                 eng[engine].tensor_copy(out=dst, in_=src)
-
-        def scale(engine, dst, src, factor):
-            if engine == "S":
-                nc.scalar.activation(out=dst, in_=src, func=COPY, scale=factor)
-            else:
-                eng[engine].tensor_scalar(out=dst, in0=src, scalar1=factor, scalar2=0.0, op0=MULT, op1=ADD)
 
         def load_x(i):
             rows = x[LAG + GROUP * i : LAG + GROUP * (i + 1), :]
@@ -308,12 +312,8 @@ def tile_lag_channel_mix_s2_kernel(tc, x, e, a, c, w, v, bias, out):
             for g in range(2):
                 for u in range(2):
                     nc.tensor.transpose(bank[:, 2 * g + u, :], words[:, 256 * g + u : 256 * (g + 1) : 2], ident[:])
-            halves = bank[:].rearrange("p q r -> p (q r)").bitcast(BF16)
-            halves = halves.rearrange("p (q b t e) -> p q e b t", q=4, t=RUN, e=2)
-            for g in range(2):
-                for s in range(4):
-                    scale(engine, ax[g][:, 0 : LAG // RUN, s, :], halves[:, 2 * g + s // 2, s % 2, 0 : LAG // RUN, :],
-                          a32[:, 4 * g + s : 4 * g + s + 1])
+            for q in range(4):
+                copy(engine, xw[q][:, 0:LAG], bank[:, q, 0:LAG])
 
         def turn(i):
             for g in range(2):
@@ -324,26 +324,29 @@ def tile_lag_channel_mix_s2_kernel(tc, x, e, a, c, w, v, bias, out):
                     for u in range(2):
                         nc.tensor.transpose(bank[:, u, P * s : P * (s + 1)], words[:, 256 * g + u : 256 * (g + 1) : 2], ident[:])
 
-        def lagged(i, g):
-            halves = live["xt", i, g][:].rearrange("p u r -> p (u r)").bitcast(BF16)
-            halves = halves.rearrange("p (u b t e) -> p u e b t", u=2, t=RUN, e=2)
-            first = (LAG + GROUP * i) // RUN
-            count = min(GROUP // RUN, T // RUN - first)
-            for s in range(4):
-                scale("S", ax[g][:, first : first + count, s, :], halves[:, s // 2, s % 2, 0:count, :],
-                      a32[:, 4 * g + s : 4 * g + s + 1])
+        def keep_words(i, g):
+            first = LAG + GROUP * i
+            count = min(GROUP, T - first)
+            for u in range(2):
+                nc.scalar.copy(out=xw[2 * g + u][:, first : first + count], in_=live["xt", i, g][:, u, 0:count])
 
         def mix_m(i, g):
+            rows = work.tile([P, 4, GROUP], BF16, name="m_rows", bufs=4)
+            live["mrows", i, g] = rows
+            now = live["xt", i, g][:].rearrange("p u r -> p (u r)").bitcast(BF16).rearrange("p (u t e) -> p u e t", u=2, e=2)
+            for s in range(4):
+                past = xw[2 * g + s // 2][:].bitcast(BF16).rearrange("p (t e) -> p e t", e=2)
+                nc.vector.scalar_tensor_tensor(
+                    out=rows[:, s, :], in0=past[:, s % 2, GROUP * i : GROUP * (i + 1)], scalar=a_bf[:, g, s : s + 1],
+                    in1=now[:, s // 2, s % 2, :], op0=MULT, op1=ADD)
+
+        def weave(engine, dst, src):
+            copy(engine, dst.rearrange("p (c i t) -> p c t i", i=4, t=4), src.rearrange("p t (c i) -> p c t i", i=4))
+
+        def weave_m(i, g, engine):
             if g == 0:
                 live["m", i] = work.tile([P, 2, 4 * GROUP], BF16, name="m_il", align_bytes=64, bufs=2)
-            halves = live["xt", i, g][:].rearrange("p u r -> p (u r)").bitcast(BF16)
-            first = GROUP * i // RUN
-            nc.vector.tensor_tensor(
-                out=live["m", i][:, g, :].rearrange("p (b t u e) -> p b t u e", t=RUN, u=2, e=2),
-                in0=halves.rearrange("p (u b t e) -> p b t u e", u=2, t=RUN, e=2),
-                in1=ax[g][:, first : first + GROUP // RUN, :, :].rearrange("p b (u e) t -> p b t u e", e=2),
-                op=ADD,
-            )
+            weave(engine, live["m", i][:, g, :], live["mrows", i, g][:])
 
         def quant_m(i):
             nc.vector.quantize_mx(out=mcodes[i][:].bitcast(E4), scales=mscales[i][:],
@@ -353,17 +356,24 @@ def tile_lag_channel_mix_s2_kernel(tc, x, e, a, c, w, v, bias, out):
             live["ce", i] = work.tile([P, 4, GROUP], F32, name="ce")
             off = GROUP * (i % 2)
             for j in range(4):
-                scale(engine, live["ce", i][:, j, :], es[i // 2][:, j, off : off + GROUP], c32[:, j : j + 1])
+                nc.gpsimd.tensor_scalar(out=live["ce", i][:, j, :], in0=es[i // 2][:, j, off : off + GROUP],
+                                        scalar1=c_bf[:, j : j + 1], scalar2=0.0, op0=MULT, op1=ADD)
 
         def mix_r(i, engine):
-            live["r", i] = work.tile([P, 4 * GROUP], BF16, name="r_il", align_bytes=64, bufs=1)
-            off = GROUP * (i % 2) + 1
-            eng[engine].tensor_tensor(
-                out=live["r", i][:].rearrange("p (t j) -> p t j", j=4),
-                in0=es[i // 2][:, :, off : off + GROUP].rearrange("p j t -> p t j"),
-                in1=live["ce", i][:].rearrange("p j t -> p t j"),
-                op=ADD,
-            )
+            rows = work.tile([P, 4, GROUP], BF16, name="r_rows", bufs=8)
+            live["rrows", i] = rows
+            off = GROUP * (i % 2)
+            if engine == "G":
+                nc.gpsimd.tensor_tensor(out=rows[:], in0=es[i // 2][:, :, off + 1 : off + 1 + GROUP], in1=live["ce", i][:], op=ADD)
+            else:
+                for j in range(4):
+                    nc.vector.scalar_tensor_tensor(
+                        out=rows[:, j, :], in0=es[i // 2][:, j, off : off + GROUP], scalar=c_bf[:, j : j + 1],
+                        in1=es[i // 2][:, j, off + 1 : off + 1 + GROUP], op0=MULT, op1=ADD)
+
+        def weave_r(i, engine):
+            live["r", i] = work.tile([P, 4 * GROUP], BF16, name="r_il", align_bytes=64, bufs=2)
+            weave(engine, live["r", i][:], live["rrows", i][:])
 
         def quant_r(i):
             nc.vector.quantize_mx(out=rcodes[i][:].bitcast(E5), scales=rscales[i][:], in_=live["r", i][:])
@@ -408,7 +418,7 @@ def tile_lag_channel_mix_s2_kernel(tc, x, e, a, c, w, v, bias, out):
             row = GROUP * i + P * s
             nc.sync.dma_start(out=out[row : row + P, HALF * h : HALF * (h + 1)], in_=live["y", i, s, h][:])
 
-        steps = {"Lx": load_x, "Le": load_e, "Lw": load_w, "B": spread_bias, "H": history, "T": turn, "A": lagged,
+        steps = {"Lx": load_x, "Le": load_e, "Lw": load_w, "B": spread_bias, "H": history, "T": turn, "K": keep_words, "J": weave_m, "JR": weave_r,
                  "M": mix_m, "Qm": quant_m, "C": scale_e, "R": mix_r, "Qr": quant_r, "I": weave_w, "Qw": quant_w,
                  "X": multiply, "E": finish, "F": empty, "Gb": add_bias, "S": store}
         for step in ORDER:

@@ -10,416 +10,312 @@ F32 = mybir.dt.float32
 BF16 = mybir.dt.bfloat16
 U32 = mybir.dt.uint32
 U8 = mybir.dt.uint8
-E4 = mybir.dt.float8_e4m3fn_x4
-E5 = mybir.dt.float8_e5m2_x4
+E4M3 = mybir.dt.float8_e4m3fn_x4
+E5M2 = mybir.dt.float8_e5m2_x4
 ADD = mybir.AluOpType.add
 MULT = mybir.AluOpType.mult
 
 P = 128
+PACK = 4
+K_PASS = P * PACK
+HALF = 512
 GROUP = 256
 GROUPS = T // GROUP
-HALF = 512
-ECH = 512
-EROW = 528
-
-ORDER = [
-    ("Le", 0,),
-    ("Lw", 0, 0,),
-    ("Lw", 1, 0,),
-    ("Lx", 0,),
-    ("Lw", 2, 0,),
-    ("Le", 1,),
-    ("Lw", 0, 1,),
-    ("Lx", 1,),
-    ("Lw", 1, 1,),
-    ("Lw", 2, 1,),
-    ("Le", 2,),
-    ("Lx", 2,),
-    ("Le", 3,),
-    ("Lx", 3,),
-    ("Lx", 4,),
-    ("Lx", 5,),
-    ("Lx", 6,),
-    ("Lx", 7,),
-    ("B", "S",),
-    ("H", "S",),
-    ("R", 0, "V",),
-    ("R", 1, "V",),
-    ("I", 0, 0, "S",),
-    ("I", 1, 0, "V",),
-    ("JR", 0, "S",),
-    ("T", 0,),
-    ("K", 0, 0,),
-    ("K", 0, 1,),
-    ("Qw", 0, 0,),
-    ("Qw", 1, 0,),
-    ("Qr", 0,),
-    ("M", 0, 0,),
-    ("M", 0, 1,),
-    ("I", 2, 0, "S",),
-    ("R", 2, "V",),
-    ("R", 3, "V",),
-    ("Qw", 2, 0,),
-    ("T", 1,),
-    ("J", 0, 0, "S",),
-    ("J", 0, 1, "S",),
-    ("K", 1, 0,),
-    ("K", 1, 1,),
-    ("I", 0, 1, "V",),
-    ("I", 1, 1, "S",),
-    ("Qm", 0,),
-    ("M", 1, 0,),
-    ("M", 1, 1,),
-    ("T", 2,),
-    ("Qw", 0, 1,),
-    ("I", 2, 1, "S",),
-    ("R", 4, "V",),
-    ("K", 2, 0,),
-    ("K", 2, 1,),
-    ("Qw", 1, 1,),
-    ("R", 5, "V",),
-    ("Qw", 2, 1,),
-    ("T", 3,),
-    ("X", 0, 0, 0,),
-    ("X", 0, 1, 0,),
-    ("X", 0, 0, 1,),
-    ("X", 0, 1, 1,),
-    ("J", 1, 0, "S",),
-    ("J", 1, 1, "S",),
-    ("JR", 1, "S",),
-    ("K", 3, 0,),
-    ("K", 3, 1,),
-    ("M", 2, 0,),
-    ("E", 0, 0, 0,),
-    ("S", 0, 0, 0,),
-    ("M", 2, 1,),
-    ("E", 0, 1, 0,),
-    ("S", 0, 1, 0,),
-    ("Qm", 1,),
-    ("Qr", 1,),
-    ("T", 4,),
-    ("E", 0, 0, 1,),
-    ("S", 0, 0, 1,),
-    ("E", 0, 1, 1,),
-    ("S", 0, 1, 1,),
-    ("X", 1, 0, 0,),
-    ("X", 1, 1, 0,),
-    ("X", 1, 0, 1,),
-    ("X", 1, 1, 1,),
-    ("J", 2, 0, "S",),
-    ("J", 2, 1, "S",),
-    ("JR", 2, "S",),
-    ("K", 4, 0,),
-    ("K", 4, 1,),
-    ("M", 3, 0,),
-    ("E", 1, 0, 0,),
-    ("S", 1, 0, 0,),
-    ("M", 3, 1,),
-    ("E", 1, 1, 0,),
-    ("S", 1, 1, 0,),
-    ("Qm", 2,),
-    ("Qr", 2,),
-    ("T", 5,),
-    ("E", 1, 0, 1,),
-    ("S", 1, 0, 1,),
-    ("E", 1, 1, 1,),
-    ("S", 1, 1, 1,),
-    ("X", 2, 0, 0,),
-    ("X", 2, 1, 0,),
-    ("X", 2, 0, 1,),
-    ("X", 2, 1, 1,),
-    ("J", 3, 0, "S",),
-    ("J", 3, 1, "S",),
-    ("JR", 3, "S",),
-    ("K", 5, 0,),
-    ("K", 5, 1,),
-    ("M", 4, 0,),
-    ("E", 2, 0, 0,),
-    ("S", 2, 0, 0,),
-    ("M", 4, 1,),
-    ("R", 6, "V",),
-    ("E", 2, 1, 0,),
-    ("S", 2, 1, 0,),
-    ("Qm", 3,),
-    ("Qr", 3,),
-    ("T", 6,),
-    ("E", 2, 0, 1,),
-    ("S", 2, 0, 1,),
-    ("E", 2, 1, 1,),
-    ("S", 2, 1, 1,),
-    ("X", 3, 0, 0,),
-    ("X", 3, 1, 0,),
-    ("X", 3, 0, 1,),
-    ("X", 3, 1, 1,),
-    ("J", 4, 0, "S",),
-    ("J", 4, 1, "S",),
-    ("JR", 4, "S",),
-    ("K", 6, 0,),
-    ("K", 6, 1,),
-    ("M", 5, 0,),
-    ("E", 3, 0, 0,),
-    ("S", 3, 0, 0,),
-    ("M", 5, 1,),
-    ("R", 7, "V",),
-    ("E", 3, 1, 0,),
-    ("S", 3, 1, 0,),
-    ("Qm", 4,),
-    ("Qr", 4,),
-    ("T", 7,),
-    ("E", 3, 0, 1,),
-    ("S", 3, 0, 1,),
-    ("E", 3, 1, 1,),
-    ("S", 3, 1, 1,),
-    ("X", 4, 0, 0,),
-    ("X", 4, 1, 0,),
-    ("X", 4, 0, 1,),
-    ("X", 4, 1, 1,),
-    ("J", 5, 0, "S",),
-    ("J", 5, 1, "S",),
-    ("JR", 5, "S",),
-    ("K", 7, 0,),
-    ("K", 7, 1,),
-    ("M", 6, 0,),
-    ("E", 4, 0, 0,),
-    ("S", 4, 0, 0,),
-    ("M", 6, 1,),
-    ("E", 4, 1, 0,),
-    ("S", 4, 1, 0,),
-    ("Qm", 5,),
-    ("Qr", 5,),
-    ("E", 4, 0, 1,),
-    ("S", 4, 0, 1,),
-    ("E", 4, 1, 1,),
-    ("S", 4, 1, 1,),
-    ("X", 5, 0, 0,),
-    ("X", 5, 1, 0,),
-    ("X", 5, 0, 1,),
-    ("X", 5, 1, 1,),
-    ("J", 6, 0, "S",),
-    ("J", 6, 1, "S",),
-    ("JR", 6, "S",),
-    ("M", 7, 0,),
-    ("E", 5, 0, 0,),
-    ("S", 5, 0, 0,),
-    ("M", 7, 1,),
-    ("E", 5, 1, 0,),
-    ("S", 5, 1, 0,),
-    ("Qm", 6,),
-    ("Qr", 6,),
-    ("E", 5, 0, 1,),
-    ("S", 5, 0, 1,),
-    ("E", 5, 1, 1,),
-    ("S", 5, 1, 1,),
-    ("X", 6, 0, 0,),
-    ("X", 6, 1, 0,),
-    ("X", 6, 0, 1,),
-    ("X", 6, 1, 1,),
-    ("J", 7, 0, "S",),
-    ("J", 7, 1, "S",),
-    ("JR", 7, "S",),
-    ("E", 6, 0, 0,),
-    ("S", 6, 0, 0,),
-    ("E", 6, 1, 0,),
-    ("S", 6, 1, 0,),
-    ("Qm", 7,),
-    ("Qr", 7,),
-    ("E", 6, 0, 1,),
-    ("S", 6, 0, 1,),
-    ("E", 6, 1, 1,),
-    ("S", 6, 1, 1,),
-    ("X", 7, 0, 0,),
-    ("X", 7, 1, 0,),
-    ("X", 7, 0, 1,),
-    ("X", 7, 1, 1,),
-    ("E", 7, 0, 0,),
-    ("S", 7, 0, 0,),
-    ("E", 7, 1, 0,),
-    ("S", 7, 1, 0,),
-    ("E", 7, 0, 1,),
-    ("S", 7, 0, 1,),
-    ("E", 7, 1, 1,),
-    ("S", 7, 1, 1,),
-]
+E_CHUNK = 512
+E_PITCH = 528
+SPANS = [(0, 256), (256, 256), (512, 512), (1024, 512), (1536, 512)]
+ACC_BANKS = 4
 
 
 def tile_lag_channel_mix_s2_kernel(tc, x, e, a, c, w, v, bias, out):
     nc = tc.nc
     with ExitStack() as ctx:
         keep = ctx.enter_context(tc.tile_pool(name="keep", bufs=1))
-        work = ctx.enter_context(tc.tile_pool(name="work", bufs=2))
-        psum = ctx.enter_context(tc.psum_pool(name="psum", bufs=2))
+        psum = ctx.enter_context(tc.psum_pool(name="psum", bufs=1))
         ctx.enter_context(tc.manual_schedule())
-        eng = {"V": nc.vector, "S": nc.scalar, "G": nc.gpsimd, "SP": nc.sync}
 
         ident = keep.tile([P, P], F32, name="ident")
         hist = keep.tile([P, C], BF16, name="hist")
-        a_bf = keep.tile([P, 2, 4], BF16, name="a_bf")
-        c_bf = keep.tile([P, 4], BF16, name="c_bf")
-        b_bf = keep.tile([P, 8], BF16, name="b_bf")
-        bias_bc = keep.tile([P, N], BF16, name="bias_bc")
-        xw = [keep.tile([P, T], F32, name="xw%d" % q) for q in range(4)]
-        xs = [keep.tile([P, 2, C], BF16, name="x%d" % i) for i in range(GROUPS)]
-        es = [keep.tile([P, 4, EROW], BF16, name="e%d" % i) for i in range(T // ECH)]
-        wraw, wcodes, wscales = {}, {}, {}
+        a_sb = keep.tile([P, 2, PACK], BF16, name="a_sb")
+        c_sb = keep.tile([P, PACK], BF16, name="c_sb")
+        bias_sb = keep.tile([P, N // P], BF16, name="bias_sb")
+        bias_all = keep.tile([P, N], BF16, name="bias_all")
+        x_words = [keep.tile([P, T], F32, name="x_words%d" % q) for q in range(4)]
+        e_sb = [keep.tile([P, PACK, E_PITCH], BF16, name="e_sb%d" % i) for i in range(T // E_CHUNK)]
+        w_codes, w_scales = {}, {}
         for g in range(3):
             for h in range(2):
-                wraw[g, h] = keep.tile([P, 4, HALF], BF16, name="wraw%d%d" % (g, h))
-                wcodes[g, h] = keep.tile([P, HALF], U32, name="wcodes%d%d" % (g, h), align_bytes=64)
-                wscales[g, h] = keep.tile([P, HALF], U8, name="wscales%d%d" % (g, h), align_bytes=64)
-        mcodes = [keep.tile([P, 2 * GROUP], U32, name="mcodes%d" % i, align_bytes=64) for i in range(GROUPS)]
-        mscales = [keep.tile([P, 2 * GROUP], U8, name="mscales%d" % i, align_bytes=64) for i in range(GROUPS)]
-        rcodes = [keep.tile([P, GROUP], U32, name="rcodes%d" % i, align_bytes=64) for i in range(GROUPS)]
-        rscales = [keep.tile([P, GROUP], U8, name="rscales%d" % i, align_bytes=64) for i in range(GROUPS)]
-        live = {}
+                w_codes[g, h] = keep.tile([P, HALF], U32, name="w_codes%d%d" % (g, h), align_bytes=64)
+                w_scales[g, h] = keep.tile([P, HALF], U8, name="w_scales%d%d" % (g, h), align_bytes=64)
+        m_codes = [keep.tile([P, 2 * GROUP], U32, name="m_codes%d" % i, align_bytes=64) for i in range(GROUPS)]
+        m_scales = [keep.tile([P, 2 * GROUP], U8, name="m_scales%d" % i, align_bytes=64) for i in range(GROUPS)]
+        r_codes = [keep.tile([P, GROUP], U32, name="r_codes%d" % i, align_bytes=64) for i in range(GROUPS)]
+        r_scales = [keep.tile([P, GROUP], U8, name="r_scales%d" % i, align_bytes=64) for i in range(GROUPS)]
+        x_sb, w_rows, w_woven, x_bank, m_rows, m_woven = {}, {}, {}, {}, {}, {}
+        scaled_e, r_rows, r_woven, acc = {}, {}, {}, {}
+
+        def load_x(i):
+            x_sb[i] = keep.tile([P, 2, C], BF16, name="x_sb", bufs=6)
+            rows = x[LAG + GROUP * i : LAG + GROUP * (i + 1), :]
+            nc.sync.dma_start(out=x_sb[i][:], in_=rows.rearrange("(s p) c -> p s c", p=P))
+
+        def load_e(i):
+            src = e.rearrange("(p j) t -> p j t", j=PACK)
+            nc.sync.dma_start(out=e_sb[i][:, :, 0 : E_CHUNK + 1], in_=src[:, :, E_CHUNK * i : E_CHUNK * (i + 1) + 1])
+
+        def load_w(g, h):
+            w_rows[g, h] = keep.tile([P, PACK, HALF], BF16, name="w_rows", tag="w_rows%d%d" % (g, h), bufs=1, align_bytes=64)
+            rows = w[K_PASS * g : K_PASS * (g + 1), :] if g < 2 else v
+            src = rows.rearrange("(p j) n -> p j n", j=PACK)
+            nc.sync.dma_start(out=w_rows[g, h][:], in_=src[:, :, HALF * h : HALF * (h + 1)])
+
+        def weave(copy, dst, src):
+            copy(out=dst.rearrange("p (c i j) -> p c j i", i=4, j=PACK), in_=src.rearrange("p j (c i) -> p c j i", i=4))
+
+        def spread_bias():
+            bank = psum.tile([P, 4, P], F32, name="bias_bank", tag="acc", bufs=ACC_BANKS)
+            words = bias_sb[:].bitcast(F32)
+            for j in range(4):
+                nc.tensor.transpose(bank[:, j, :], words[:, j : j + 1].to_broadcast([P, P]), ident[:])
+            dst = bias_all[:].bitcast(F32).rearrange("p (n j) -> p n j", j=4)
+            nc.scalar.copy(out=dst, in_=bank[:].rearrange("p j n -> p n j"))
+
+        def every_second_word(rows, q):
+            g, u = divmod(q, 2)
+            return rows.bitcast(F32)[:, 256 * g + u : 256 * (g + 1) : 2]
+
+        def turn_history():
+            bank = psum.tile([P, 4, P], F32, name="hist_bank", tag="acc", bufs=ACC_BANKS)
+            for q in range(4):
+                nc.tensor.transpose(bank[:, q, :], every_second_word(hist[:], q), ident[:])
+            for q in range(4):
+                nc.scalar.copy(out=x_words[q][:, 0:LAG], in_=bank[:, q, 0:LAG])
+
+        def turn_x(span):
+            first, size = SPANS[span]
+            for q in range(4):
+                x_bank[span, q] = psum.tile([P, size], F32, name="x_bank%d" % q)
+                for t in range(0, size, P):
+                    i, s = divmod((first + t) // P, 2)
+                    nc.tensor.transpose(x_bank[span, q][:, t : t + P], every_second_word(x_sb[i][:, s, :], q), ident[:])
+
+        def keep_x(span):
+            first, size = SPANS[span]
+            count = min(size, T - LAG - first)
+            for q in range(4):
+                nc.scalar.copy(out=x_words[q][:, LAG + first : LAG + first + count], in_=x_bank[span, q][:, 0:count])
+
+        def mix_m(span, q):
+            first, size = SPANS[span]
+            g, u = divmod(q, 2)
+            if u == 0:
+                m_rows[span, g] = keep.tile([P, PACK, size], BF16, name="m_rows", bufs=4)
+            past = x_words[q][:].bitcast(BF16).rearrange("p (t d) -> p d t", d=2)
+            now = x_bank[span, q][:].bitcast(BF16).rearrange("p (t d) -> p d t", d=2)
+            for d in range(2):
+                j = 2 * u + d
+                nc.vector.scalar_tensor_tensor(
+                    out=m_rows[span, g][:, j, :], in0=past[:, d, first : first + size], scalar=a_sb[:, g, j : j + 1],
+                    in1=now[:, d, :], op0=MULT, op1=ADD)
+
+        def weave_m(i, g):
+            span = max(s for s in range(len(SPANS)) if SPANS[s][0] <= GROUP * i)
+            off = GROUP * i - SPANS[span][0]
+            if g == 0:
+                m_woven[i] = keep.tile([P, 2, PACK * GROUP], BF16, name="m_woven", align_bytes=64, bufs=2)
+            weave(nc.scalar.copy, m_woven[i][:, g, :], m_rows[span, g][:, :, off : off + GROUP])
+
+        def quantize_m(i):
+            nc.vector.quantize_mx(out=m_codes[i][:].bitcast(E4M3), scales=m_scales[i][:],
+                                  in_=m_woven[i][:].rearrange("p g k -> p (g k)"))
+
+        def mix_first_r():
+            rows = keep.tile([P, PACK, E_CHUNK], BF16, name="first_r_rows")
+            for j in range(PACK):
+                nc.vector.scalar_tensor_tensor(
+                    out=rows[:, j, :], in0=e_sb[0][:, j, 0:E_CHUNK], scalar=c_sb[:, j : j + 1],
+                    in1=e_sb[0][:, j, 1 : E_CHUNK + 1], op0=MULT, op1=ADD)
+            for i in range(2):
+                r_rows[i] = rows[:, :, GROUP * i : GROUP * (i + 1)]
+
+        def scale_e(i, tag="scaled_e", bufs=2):
+            scaled_e[i] = keep.tile([P, PACK, GROUP], F32, name="scaled_e", tag=tag, bufs=bufs, align_bytes=64)
+            off = GROUP * (i % 2)
+            for j in range(PACK):
+                nc.gpsimd.tensor_scalar(out=scaled_e[i][:, j, :], in0=e_sb[i // 2][:, j, off : off + GROUP],
+                                        scalar1=c_sb[:, j : j + 1], scalar2=0.0, op0=MULT, op1=ADD)
+
+        def add_r(i, tag):
+            rows = keep.tile([P, PACK, GROUP], BF16, name="r_rows", tag=tag, bufs=1, align_bytes=64)
+            off = GROUP * (i % 2) + 1
+            nc.gpsimd.tensor_tensor(out=rows[:], in0=e_sb[i // 2][:, :, off : off + GROUP], in1=scaled_e[i][:], op=ADD)
+            r_rows[i] = rows[:]
+
+        def weave_r(i):
+            r_woven[i] = keep.tile([P, PACK * GROUP], BF16, name="r_woven", tag="r_woven%d" % i, bufs=1, align_bytes=64)
+            weave(nc.scalar.copy, r_woven[i][:], r_rows[i])
+
+        def quantize_r(i):
+            nc.vector.quantize_mx(out=r_codes[i][:].bitcast(E5M2), scales=r_scales[i][:], in_=r_woven[i][:])
+
+        def weave_w(g, h, copy):
+            w_woven[g, h] = keep.tile([P, PACK * HALF], BF16, name="w_woven", tag="w_woven%d%d" % (g, h), bufs=1, align_bytes=64)
+            weave(copy, w_woven[g, h][:], w_rows[g, h][:])
+
+        def weave_w_on_gpsimd(g, h, tag):
+            w_woven[g, h] = keep.tile([P, PACK * HALF], BF16, name="w_woven", tag=tag, bufs=1, align_bytes=64)
+            nc.gpsimd.tensor_scalar(out=w_woven[g, h][:].rearrange("p (n j) -> p n j", j=PACK),
+                                    in0=w_rows[g, h][:].rearrange("p j n -> p n j"),
+                                    scalar1=1.0, scalar2=0.0, op0=MULT, op1=ADD)
+
+        def quantize_w(g, h):
+            nc.vector.quantize_mx(out=w_codes[g, h][:].bitcast(E4M3), scales=w_scales[g, h][:], in_=w_woven[g, h][:])
+
+        blocks = [(i, s, h) for h in range(2) for i in range(2) for s in range(2)]
+        blocks = blocks + [(i, s, h) for i in range(2, GROUPS) for h in range(2) for s in range(2)]
+
+        def multiply(k):
+            i, s, h = blocks[k]
+            acc[k] = psum.tile([P, HALF], F32, name="acc", tag="acc", bufs=ACC_BANKS)
+            for g in range(2):
+                cols = slice(GROUP * g + P * s, GROUP * g + P * (s + 1))
+                nc.tensor.matmul_mx(out=acc[k][:], lhsT=m_codes[i][:, cols].bitcast(E4M3), lhsT_scale=m_scales[i][:, cols],
+                                    rhs=w_codes[g, h][:].bitcast(E4M3), rhs_scale=w_scales[g, h][:],
+                                    start=(g == 0), stop=False)
+            cols = slice(P * s, P * (s + 1))
+            nc.tensor.matmul_mx(out=acc[k][:], lhsT=r_codes[i][:, cols].bitcast(E5M2), lhsT_scale=r_scales[i][:, cols],
+                                rhs=w_codes[2, h][:].bitcast(E4M3), rhs_scale=w_scales[2, h][:],
+                                start=False, stop=True)
+
+        def finish(k):
+            i, s, h = blocks[k]
+            cols = slice(HALF * h, HALF * (h + 1))
+            y = keep.tile([P, HALF], F32, name="y", bufs=6)
+            nc.vector.tensor_tensor(out=y[:], in0=acc[k][:], in1=bias_all[:, cols], op=ADD)
+            row = GROUP * i + P * s
+            nc.sync.dma_start(out=out[row : row + P, cols], in_=y[:])
+
+        def finish_and_refill(k):
+            finish(k)
+            if k + ACC_BANKS < len(blocks):
+                multiply(k + ACC_BANKS)
+
+        def weave_group(i):
+            weave_m(i, 0)
+            weave_m(i, 1)
+            weave_r(i)
+
+        def quantize_group(i):
+            quantize_m(i)
+            quantize_r(i)
 
         nc.vector.memset(hist[:], 0.0)
         make_identity(nc, ident[:])
-        nc.scalar.dma_start(out=a_bf[:], in_=a.rearrange("(g p t) -> p g t", g=2, t=4))
-        nc.scalar.dma_start(out=b_bf[:], in_=bias.rearrange("(p j) -> p j", j=8))
-        nc.scalar.dma_start(out=c_bf[:], in_=c.rearrange("(p t) -> p t", t=4))
+        nc.scalar.dma_start(out=a_sb[:], in_=a.rearrange("(g p j) -> p g j", g=2, j=PACK))
+        nc.scalar.dma_start(out=bias_sb[:], in_=bias.rearrange("(p j) -> p j", p=P))
+        nc.scalar.dma_start(out=c_sb[:], in_=c.rearrange("(p j) -> p j", j=PACK))
         nc.scalar.dma_start(out=hist[0:LAG, :], in_=x[0:LAG, :])
+        load_e(0)
+        load_x(0)
+        load_w(0, 0)
+        load_e(1)
+        load_x(1)
+        load_w(2, 0)
+        load_w(1, 0)
+        load_w(0, 1)
+        load_x(2)
+        load_x(3)
+        load_w(1, 1)
+        load_w(2, 1)
+        load_e(2)
+        load_x(4)
+        load_x(5)
+        load_e(3)
 
-        def copy(engine, dst, src):
-            if engine == "S":
-                nc.scalar.copy(out=dst, in_=src)
-            else:
-                eng[engine].tensor_copy(out=dst, in_=src)
+        spread_bias()
+        turn_history()
+        mix_first_r()
+        weave_r(0)
+        turn_x(0)
+        keep_x(0)
+        weave_w(0, 0, nc.vector.tensor_copy)
+        scale_e(2)
+        for q in range(4):
+            mix_m(0, q)
+        weave_m(0, 0)
+        turn_x(1)
+        load_x(6)
+        load_x(7)
+        keep_x(1)
+        weave_w(2, 0, nc.vector.tensor_copy)
+        weave_w_on_gpsimd(1, 0, "w_rows20")
+        weave_m(0, 1)
+        for q in range(4):
+            mix_m(1, q)
+        weave_w(0, 1, nc.scalar.copy)
+        turn_x(2)
+        quantize_w(0, 0)
+        quantize_w(2, 0)
+        quantize_r(0)
+        quantize_m(0)
+        quantize_w(1, 0)
+        quantize_w(0, 1)
 
-        def load_x(i):
-            rows = x[LAG + GROUP * i : LAG + GROUP * (i + 1), :]
-            nc.sync.dma_start(out=xs[i][:], in_=rows.rearrange("(s p) c -> p s c", p=P))
+        keep_x(2)
+        multiply(0)
+        multiply(1)
+        add_r(2, "w_woven01")
+        scale_e(3)
+        scale_e(4)
+        weave_group(1)
+        weave_w(1, 1, nc.scalar.copy)
+        mix_m(2, 0)
+        mix_m(2, 1)
+        finish(0)
+        mix_m(2, 2)
+        finish(1)
+        mix_m(2, 3)
+        turn_x(3)
+        weave_w(2, 1, nc.vector.tensor_copy)
+        quantize_group(1)
+        quantize_w(2, 1)
+        quantize_w(1, 1)
 
-        def load_e(i):
-            src = e.rearrange("(p j) t -> p j t", j=4)
-            nc.sync.dma_start(out=es[i][:, :, 0 : ECH + 1], in_=src[:, :, ECH * i : ECH * (i + 1) + 1])
+        keep_x(3)
+        for k in range(2, 2 + ACC_BANKS):
+            multiply(k)
+        add_r(3, "w_woven11")
+        add_r(4, "w_rows21")
+        scale_e(5)
+        weave_group(2)
+        mix_m(3, 0)
+        mix_m(3, 1)
+        finish_and_refill(2)
+        mix_m(3, 2)
+        finish_and_refill(3)
+        mix_m(3, 3)
+        finish(4)
+        turn_x(4)
+        quantize_group(2)
 
-        def load_w(g, h):
-            rows = w[512 * g : 512 * (g + 1), :] if g < 2 else v
-            src = rows.rearrange("(p j) n -> p j n", j=4)
-            nc.sync.dma_start(out=wraw[g, h][:], in_=src[:, :, HALF * h : HALF * (h + 1)])
+        scale_e(6, "r_woven2", 1)
+        weave_group(3)
+        keep_x(4)
+        multiply(8)
+        for k in range(5, 8):
+            finish_and_refill(k)
+        quantize_group(3)
 
-        def spread_bias(engine):
-            bank = psum.tile([P, 4, P], F32, name="bias_bank", tag="acc", bufs=4)
-            words = b_bf[:].bitcast(F32)
-            for j in range(4):
-                nc.tensor.transpose(bank[:, j, :], words[:, j : j + 1].to_broadcast([P, P]), ident[:])
-            dst = bias_bc[:].bitcast(F32).rearrange("p (n j) -> p n j", j=4)
-            copy(engine, dst, bank[:].rearrange("p j n -> p n j"))
-
-        def history(engine):
-            bank = psum.tile([P, 4, P], F32, name="hist_bank", tag="acc", bufs=4)
-            words = hist[:].bitcast(F32)
-            for g in range(2):
-                for u in range(2):
-                    nc.tensor.transpose(bank[:, 2 * g + u, :], words[:, 256 * g + u : 256 * (g + 1) : 2], ident[:])
-            for q in range(4):
-                copy(engine, xw[q][:, 0:LAG], bank[:, q, 0:LAG])
-
-        def turn(i):
-            for g in range(2):
-                bank = psum.tile([P, 2, GROUP], F32, name="xt%d" % g, tag="xt%d" % g, bufs=2)
-                live["xt", i, g] = bank
-                for s in range(2):
-                    words = xs[i][:, s, :].bitcast(F32)
-                    for u in range(2):
-                        nc.tensor.transpose(bank[:, u, P * s : P * (s + 1)], words[:, 256 * g + u : 256 * (g + 1) : 2], ident[:])
-
-        def keep_words(i, g):
-            first = LAG + GROUP * i
-            count = min(GROUP, T - first)
-            for u in range(2):
-                nc.scalar.copy(out=xw[2 * g + u][:, first : first + count], in_=live["xt", i, g][:, u, 0:count])
-
-        def mix_m(i, g):
-            rows = work.tile([P, 4, GROUP], BF16, name="m_rows", bufs=4)
-            live["mrows", i, g] = rows
-            now = live["xt", i, g][:].rearrange("p u r -> p (u r)").bitcast(BF16).rearrange("p (u t e) -> p u e t", u=2, e=2)
-            for s in range(4):
-                past = xw[2 * g + s // 2][:].bitcast(BF16).rearrange("p (t e) -> p e t", e=2)
-                nc.vector.scalar_tensor_tensor(
-                    out=rows[:, s, :], in0=past[:, s % 2, GROUP * i : GROUP * (i + 1)], scalar=a_bf[:, g, s : s + 1],
-                    in1=now[:, s // 2, s % 2, :], op0=MULT, op1=ADD)
-
-        def weave(engine, dst, src):
-            copy(engine, dst.rearrange("p (c i t) -> p c t i", i=4, t=4), src.rearrange("p t (c i) -> p c t i", i=4))
-
-        def weave_m(i, g, engine):
-            if g == 0:
-                live["m", i] = work.tile([P, 2, 4 * GROUP], BF16, name="m_il", align_bytes=64, bufs=2)
-            weave(engine, live["m", i][:, g, :], live["mrows", i, g][:])
-
-        def quant_m(i):
-            nc.vector.quantize_mx(out=mcodes[i][:].bitcast(E4), scales=mscales[i][:],
-                                  in_=live["m", i][:].rearrange("p g k -> p (g k)"))
-
-        def scale_e(i, engine):
-            live["ce", i] = work.tile([P, 4, GROUP], F32, name="ce")
-            off = GROUP * (i % 2)
-            for j in range(4):
-                nc.gpsimd.tensor_scalar(out=live["ce", i][:, j, :], in0=es[i // 2][:, j, off : off + GROUP],
-                                        scalar1=c_bf[:, j : j + 1], scalar2=0.0, op0=MULT, op1=ADD)
-
-        def mix_r(i, engine):
-            rows = work.tile([P, 4, GROUP], BF16, name="r_rows", bufs=8)
-            live["rrows", i] = rows
-            off = GROUP * (i % 2)
-            if engine == "G":
-                nc.gpsimd.tensor_tensor(out=rows[:], in0=es[i // 2][:, :, off + 1 : off + 1 + GROUP], in1=live["ce", i][:], op=ADD)
-            else:
-                for j in range(4):
-                    nc.vector.scalar_tensor_tensor(
-                        out=rows[:, j, :], in0=es[i // 2][:, j, off : off + GROUP], scalar=c_bf[:, j : j + 1],
-                        in1=es[i // 2][:, j, off + 1 : off + 1 + GROUP], op0=MULT, op1=ADD)
-
-        def weave_r(i, engine):
-            live["r", i] = work.tile([P, 4 * GROUP], BF16, name="r_il", align_bytes=64, bufs=2)
-            weave(engine, live["r", i][:], live["rrows", i][:])
-
-        def quant_r(i):
-            nc.vector.quantize_mx(out=rcodes[i][:].bitcast(E5), scales=rscales[i][:], in_=live["r", i][:])
-
-        def weave_w(g, h, engine):
-            live["w", g, h] = work.tile([P, HALF, 4], BF16, name="w_il", align_bytes=64, bufs=3)
-            copy(engine, live["w", g, h][:].rearrange("p (c i) t -> p c t i", i=4),
-                 wraw[g, h][:].rearrange("p t (c i) -> p c t i", i=4))
-
-        def quant_w(g, h):
-            nc.vector.quantize_mx(out=wcodes[g, h][:].bitcast(E4), scales=wscales[g, h][:],
-                                  in_=live["w", g, h][:].rearrange("p n t -> p (n t)"))
-
-        def multiply(i, s, h):
-            acc = psum.tile([P, HALF], F32, name="acc", tag="acc", bufs=4)
-            live["acc", i, s, h] = acc
-            for g in range(2):
-                cols = slice(GROUP * g + P * s, GROUP * g + P * (s + 1))
-                nc.tensor.matmul_mx(out=acc[:], lhsT=mcodes[i][:, cols].bitcast(E4), lhsT_scale=mscales[i][:, cols],
-                                    rhs=wcodes[g, h][:].bitcast(E4), rhs_scale=wscales[g, h][:],
-                                    start=(g == 0), stop=False)
-            cols = slice(P * s, P * (s + 1))
-            nc.tensor.matmul_mx(out=acc[:], lhsT=rcodes[i][:, cols].bitcast(E5), lhsT_scale=rscales[i][:, cols],
-                                rhs=wcodes[2, h][:].bitcast(E4), rhs_scale=wscales[2, h][:],
-                                start=False, stop=True)
-
-        def finish(i, s, h):
-            y = work.tile([P, HALF], F32, name="y", bufs=8)
-            live["y", i, s, h] = y
-            nc.vector.tensor_tensor(out=y[:], in0=live["acc", i, s, h][:], in1=bias_bc[:, HALF * h : HALF * (h + 1)], op=ADD)
-
-        def empty(i, s, h):
-            y = work.tile([P, HALF], F32, name="y", bufs=8)
-            live["y", i, s, h] = y
-            nc.scalar.copy(out=y[:], in_=live["acc", i, s, h][:])
-
-        def add_bias(i, s, h):
-            y = live["y", i, s, h]
-            nc.gpsimd.tensor_tensor(out=y[:], in0=y[:], in1=bias_bc[:, HALF * h : HALF * (h + 1)], op=ADD)
-
-        def store(i, s, h):
-            row = GROUP * i + P * s
-            nc.sync.dma_start(out=out[row : row + P, HALF * h : HALF * (h + 1)], in_=live["y", i, s, h][:])
-
-        steps = {"Lx": load_x, "Le": load_e, "Lw": load_w, "B": spread_bias, "H": history, "T": turn, "K": keep_words, "J": weave_m, "JR": weave_r,
-                 "M": mix_m, "Qm": quant_m, "C": scale_e, "R": mix_r, "Qr": quant_r, "I": weave_w, "Qw": quant_w,
-                 "X": multiply, "E": finish, "F": empty, "Gb": add_bias, "S": store}
-        for step in ORDER:
-            steps[step[0]](*step[1:])
+        for i in range(4, GROUPS):
+            if i + 1 < GROUPS:
+                add_r(i + 1, "r_woven%d" % (i - 1))
+            if i == 4:
+                scale_e(7)
+            weave_group(i)
+            for n in range(4):
+                if i < 6 and n % 2 == 0:
+                    mix_m(4, 2 * (i - 4) + n // 2)
+                finish_and_refill(4 * (i - 2) + n)
+            quantize_group(i)
+        for k in range(4 * (GROUPS - 2), len(blocks)):
+            finish_and_refill(k)

@@ -129,17 +129,17 @@ def tile_lag_channel_mix_s2_kernel(tc, x, e, a, c, w, v, bias, out):
             nc.vector.quantize_mx(out=m_codes[i][:].bitcast(E4M3), scales=m_scales[i][:],
                                   in_=m_woven[i][:].rearrange("p g k -> p (g k)"))
 
-        def mix_first_r():
-            rows = keep.tile([P, PACK, E_CHUNK], BF16, name="first_r_rows")
+        def mix_r_on_vector(chunk):
+            rows = keep.tile([P, PACK, E_CHUNK], BF16, name="chunk_r_rows")
             for j in range(PACK):
                 nc.vector.scalar_tensor_tensor(
-                    out=rows[:, j, :], in0=e_sb[0][:, j, 0:E_CHUNK], scalar=c_sb[:, j : j + 1],
-                    in1=e_sb[0][:, j, 1 : E_CHUNK + 1], op0=MULT, op1=ADD)
-            for i in range(2):
-                r_rows[i] = rows[:, :, GROUP * i : GROUP * (i + 1)]
+                    out=rows[:, j, :], in0=e_sb[chunk][:, j, 0:E_CHUNK], scalar=c_sb[:, j : j + 1],
+                    in1=e_sb[chunk][:, j, 1 : E_CHUNK + 1], op0=MULT, op1=ADD)
+            for n in range(2):
+                r_rows[2 * chunk + n] = rows[:, :, GROUP * n : GROUP * (n + 1)]
 
-        def scale_e(i, tag="scaled_e", bufs=2):
-            scaled_e[i] = keep.tile([P, PACK, GROUP], F32, name="scaled_e", tag=tag, bufs=bufs, align_bytes=64)
+        def scale_e(i):
+            scaled_e[i] = keep.tile([P, PACK, GROUP], F32, name="scaled_e", bufs=2)
             off = GROUP * (i % 2)
             for j in range(PACK):
                 nc.gpsimd.tensor_scalar(out=scaled_e[i][:, j, :], in0=e_sb[i // 2][:, j, off : off + GROUP],
@@ -162,11 +162,11 @@ def tile_lag_channel_mix_s2_kernel(tc, x, e, a, c, w, v, bias, out):
             w_woven[g, h] = keep.tile([P, PACK * HALF], BF16, name="w_woven", tag="w_woven%d%d" % (g, h), bufs=1, align_bytes=64)
             weave(copy, w_woven[g, h][:], w_rows[g, h][:])
 
-        def weave_w_on_gpsimd(g, h, tag):
-            w_woven[g, h] = keep.tile([P, PACK * HALF], BF16, name="w_woven", tag=tag, bufs=1, align_bytes=64)
-            nc.gpsimd.tensor_scalar(out=w_woven[g, h][:].rearrange("p (n j) -> p n j", j=PACK),
-                                    in0=w_rows[g, h][:].rearrange("p j n -> p n j"),
+        def weave_on_gpsimd(src, tag):
+            dst = keep.tile([P, PACK * src.shape[2]], BF16, name="woven", tag=tag, bufs=1, align_bytes=64)
+            nc.gpsimd.tensor_scalar(out=dst[:].rearrange("p (n j) -> p n j", j=PACK), in0=src.rearrange("p j n -> p n j"),
                                     scalar1=1.0, scalar2=0.0, op0=MULT, op1=ADD)
+            return dst
 
         def quantize_w(g, h):
             nc.vector.quantize_mx(out=w_codes[g, h][:].bitcast(E4M3), scales=w_scales[g, h][:], in_=w_woven[g, h][:])
@@ -195,10 +195,11 @@ def tile_lag_channel_mix_s2_kernel(tc, x, e, a, c, w, v, bias, out):
             row = GROUP * i + P * s
             nc.sync.dma_start(out=out[row : row + P, cols], in_=y[:])
 
-        def finish_and_refill(k):
+        def finish_and_refill(k, quantized):
             finish(k)
-            if k + ACC_BANKS < len(blocks):
-                multiply(k + ACC_BANKS)
+            later = k + ACC_BANKS
+            if later < len(blocks) and blocks[later][0] < quantized:
+                multiply(later)
 
         def weave_group(i):
             weave_m(i, 0)
@@ -218,15 +219,15 @@ def tile_lag_channel_mix_s2_kernel(tc, x, e, a, c, w, v, bias, out):
         load_e(0)
         load_x(0)
         load_w(0, 0)
-        load_e(1)
         load_x(1)
-        load_w(2, 0)
         load_w(1, 0)
+        load_w(2, 0)
         load_w(0, 1)
         load_x(2)
         load_x(3)
-        load_w(1, 1)
         load_w(2, 1)
+        load_w(1, 1)
+        load_e(1)
         load_e(2)
         load_x(4)
         load_x(5)
@@ -234,40 +235,40 @@ def tile_lag_channel_mix_s2_kernel(tc, x, e, a, c, w, v, bias, out):
 
         spread_bias()
         turn_history()
-        mix_first_r()
+        mix_r_on_vector(0)
         weave_r(0)
         turn_x(0)
         keep_x(0)
+        weave_r(1)
         weave_w(0, 0, nc.vector.tensor_copy)
-        scale_e(2)
+        w_woven[1, 0] = weave_on_gpsimd(w_rows[1, 0][:], "w_rows00")
         for q in range(4):
             mix_m(0, q)
-        weave_m(0, 0)
         turn_x(1)
         load_x(6)
         load_x(7)
         keep_x(1)
-        weave_w(2, 0, nc.vector.tensor_copy)
-        weave_w_on_gpsimd(1, 0, "w_rows20")
-        weave_m(0, 1)
         for q in range(4):
             mix_m(1, q)
-        weave_w(0, 1, nc.scalar.copy)
         turn_x(2)
+        weave_m(0, 0)
+        weave_m(0, 1)
+        weave_w(0, 1, nc.scalar.copy)
+        weave_w(2, 0, nc.vector.tensor_copy)
         quantize_w(0, 0)
-        quantize_w(2, 0)
         quantize_r(0)
         quantize_m(0)
         quantize_w(1, 0)
+        quantize_w(2, 0)
         quantize_w(0, 1)
 
         keep_x(2)
         multiply(0)
         multiply(1)
-        add_r(2, "w_woven01")
-        scale_e(3)
+        w_woven[2, 1] = weave_on_gpsimd(w_rows[2, 1][:], "w_woven01")
         scale_e(4)
-        weave_group(1)
+        weave_m(1, 0)
+        weave_m(1, 1)
         weave_w(1, 1, nc.scalar.copy)
         mix_m(2, 0)
         mix_m(2, 1)
@@ -276,7 +277,7 @@ def tile_lag_channel_mix_s2_kernel(tc, x, e, a, c, w, v, bias, out):
         finish(1)
         mix_m(2, 3)
         turn_x(3)
-        weave_w(2, 1, nc.vector.tensor_copy)
+        mix_r_on_vector(1)
         quantize_group(1)
         quantize_w(2, 1)
         quantize_w(1, 1)
@@ -284,38 +285,41 @@ def tile_lag_channel_mix_s2_kernel(tc, x, e, a, c, w, v, bias, out):
         keep_x(3)
         for k in range(2, 2 + ACC_BANKS):
             multiply(k)
-        add_r(3, "w_woven11")
-        add_r(4, "w_rows21")
+        r_woven[2] = weave_on_gpsimd(r_rows[2], "w_woven11")
+        add_r(4, "w_rows20")
         scale_e(5)
-        weave_group(2)
+        weave_m(2, 0)
+        weave_m(2, 1)
+        weave_group(3)
         mix_m(3, 0)
         mix_m(3, 1)
-        finish_and_refill(2)
+        finish_and_refill(2, 2)
         mix_m(3, 2)
-        finish_and_refill(3)
+        finish_and_refill(3, 2)
         mix_m(3, 3)
         finish(4)
+        finish(5)
         turn_x(4)
-        quantize_group(2)
-
-        scale_e(6, "r_woven2", 1)
-        weave_group(3)
         keep_x(4)
+        quantize_group(2)
         multiply(8)
-        for k in range(5, 8):
-            finish_and_refill(k)
+        multiply(9)
         quantize_group(3)
 
+        ends = {3: 6, 4: 12, 5: 16, 6: 21, 7: 24}
         for i in range(4, GROUPS):
             if i + 1 < GROUPS:
                 add_r(i + 1, "r_woven%d" % (i - 1))
-            if i == 4:
-                scale_e(7)
+            if i + 2 < GROUPS:
+                scale_e(i + 2)
             weave_group(i)
-            for n in range(4):
-                if i < 6 and n % 2 == 0:
-                    mix_m(4, 2 * (i - 4) + n // 2)
-                finish_and_refill(4 * (i - 2) + n)
+            for k in range(ends[i - 1], ends[i]):
+                if 8 <= k < 16 and k % 2 == 0:
+                    mix_m(4, (k - 8) // 2)
+                finish_and_refill(k, i)
             quantize_group(i)
-        for k in range(4 * (GROUPS - 2), len(blocks)):
-            finish_and_refill(k)
+            for k in range(ends[i - 1], ends[i]):
+                if blocks[k + ACC_BANKS][0] == i:
+                    multiply(k + ACC_BANKS)
+        for k in range(ends[GROUPS - 1], len(blocks)):
+            finish_and_refill(k, GROUPS)

@@ -21,7 +21,7 @@ K_PASS = P * PACK
 HALF = 512
 GROUP = 256
 GROUPS = T // GROUP
-E_CHUNK = 512
+E_CHUNK = 2 * GROUP
 E_PITCH = 528
 SPANS = [(0, 256), (256, 256), (512, 512), (1024, 512), (1536, 512)]
 ACC_BANKS = 4
@@ -82,7 +82,8 @@ def tile_lag_channel_mix_s2_kernel(tc, x, e, a, c, w, v, bias, out):
 
         def every_second_word(rows, q):
             g, u = divmod(q, 2)
-            return rows.bitcast(F32)[:, 256 * g + u : 256 * (g + 1) : 2]
+            words_a_pass = K_PASS // 2
+            return rows.bitcast(F32)[:, words_a_pass * g + u : words_a_pass * (g + 1) : 2]
 
         def turn_history():
             bank = psum.tile([P, 4, P], F32, name="hist_bank", tag="acc", bufs=ACC_BANKS)
@@ -189,11 +190,13 @@ def tile_lag_channel_mix_s2_kernel(tc, x, e, a, c, w, v, bias, out):
 
         def finish(k):
             i, s, h = blocks[k]
-            cols = slice(HALF * h, HALF * (h + 1))
-            y = keep.tile([P, HALF], F32, name="y", bufs=6)
-            nc.vector.tensor_tensor(out=y[:], in0=acc[k][:], in1=bias_all[:, cols], op=ADD)
             row = GROUP * i + P * s
-            nc.sync.dma_start(out=out[row : row + P, cols], in_=y[:])
+            width = HALF // 2 if k == len(blocks) - 1 else HALF
+            for n in range(0, HALF, width):
+                cols = slice(HALF * h + n, HALF * h + n + width)
+                y = keep.tile([P, width], F32, name="y", bufs=12)
+                nc.vector.tensor_tensor(out=y[:], in0=acc[k][:, n : n + width], in1=bias_all[:, cols], op=ADD)
+                nc.sync.dma_start(out=out[row : row + P, cols], in_=y[:])
 
         def finish_and_refill(k, quantized):
             finish(k)
@@ -219,12 +222,12 @@ def tile_lag_channel_mix_s2_kernel(tc, x, e, a, c, w, v, bias, out):
         load_e(0)
         load_x(0)
         load_w(0, 0)
-        load_x(1)
         load_w(1, 0)
+        load_x(1)
         load_w(2, 0)
-        load_w(0, 1)
         load_x(2)
         load_x(3)
+        load_w(0, 1)
         load_w(2, 1)
         load_w(1, 1)
         load_e(1)
@@ -242,6 +245,7 @@ def tile_lag_channel_mix_s2_kernel(tc, x, e, a, c, w, v, bias, out):
         weave_r(1)
         weave_w(0, 0, nc.vector.tensor_copy)
         w_woven[1, 0] = weave_on_gpsimd(w_rows[1, 0][:], "w_rows00")
+        w_woven[2, 0] = weave_on_gpsimd(w_rows[2, 0][:], "w_woven20")
         for q in range(4):
             mix_m(0, q)
         turn_x(1)
@@ -253,20 +257,18 @@ def tile_lag_channel_mix_s2_kernel(tc, x, e, a, c, w, v, bias, out):
         turn_x(2)
         weave_m(0, 0)
         weave_m(0, 1)
-        weave_w(0, 1, nc.scalar.copy)
-        weave_w(2, 0, nc.vector.tensor_copy)
         quantize_w(0, 0)
         quantize_r(0)
         quantize_m(0)
         quantize_w(1, 0)
         quantize_w(2, 0)
-        quantize_w(0, 1)
 
         keep_x(2)
         multiply(0)
         multiply(1)
-        w_woven[2, 1] = weave_on_gpsimd(w_rows[2, 1][:], "w_woven01")
+        w_woven[2, 1] = weave_on_gpsimd(w_rows[2, 1][:], "w_woven20")
         scale_e(4)
+        weave_w(0, 1, nc.scalar.copy)
         weave_m(1, 0)
         weave_m(1, 1)
         weave_w(1, 1, nc.scalar.copy)
@@ -277,6 +279,7 @@ def tile_lag_channel_mix_s2_kernel(tc, x, e, a, c, w, v, bias, out):
         finish(1)
         mix_m(2, 3)
         turn_x(3)
+        quantize_w(0, 1)
         mix_r_on_vector(1)
         quantize_group(1)
         quantize_w(2, 1)
@@ -302,24 +305,31 @@ def tile_lag_channel_mix_s2_kernel(tc, x, e, a, c, w, v, bias, out):
         turn_x(4)
         keep_x(4)
         quantize_group(2)
-        multiply(8)
-        multiply(9)
+        multiply(4 + ACC_BANKS)
+        multiply(5 + ACC_BANKS)
         quantize_group(3)
 
-        ends = {3: 6, 4: 12, 5: 16, 6: 21, 7: 24}
+        def finished_before(i):
+            if i == 3:
+                return 6
+            beside_last_add = 1 if i + 1 == GROUPS - 1 else 0
+            return 4 * (i - 1) + beside_last_add
+
+        last_span, first_of_group_2, first_of_group_4 = len(SPANS) - 1, 8, 16
         for i in range(4, GROUPS):
             if i + 1 < GROUPS:
                 add_r(i + 1, "r_woven%d" % (i - 1))
             if i + 2 < GROUPS:
                 scale_e(i + 2)
             weave_group(i)
-            for k in range(ends[i - 1], ends[i]):
-                if 8 <= k < 16 and k % 2 == 0:
-                    mix_m(4, (k - 8) // 2)
+            step = range(finished_before(i - 1), finished_before(i))
+            for k in step:
+                if first_of_group_2 <= k < first_of_group_4 and k % 2 == 0:
+                    mix_m(last_span, (k - first_of_group_2) // 2)
                 finish_and_refill(k, i)
             quantize_group(i)
-            for k in range(ends[i - 1], ends[i]):
+            for k in step:
                 if blocks[k + ACC_BANKS][0] == i:
                     multiply(k + ACC_BANKS)
-        for k in range(ends[GROUPS - 1], len(blocks)):
+        for k in range(finished_before(GROUPS - 1), len(blocks)):
             finish_and_refill(k, GROUPS)

from contextlib import ExitStack

import concourse.mybir as mybir
from concourse.masks import make_identity

T, C, D, N, LAG = 2048, 1024, 512, 1024, 24
FLOPS = 2 * T * (C + D) * N

F32 = mybir.dt.float32
BF16 = mybir.dt.bfloat16
U32 = mybir.dt.uint32
U8 = mybir.dt.uint8
E4M3 = mybir.dt.float8_e4m3fn_x4
E5M2 = mybir.dt.float8_e5m2_x4
ADD = mybir.AluOpType.add
MULT = mybir.AluOpType.mult

P = 128
PACK = 4
K_PASS = P * PACK
HALF = 512
GROUP = 256
GROUPS = T // GROUP
E_CHUNK = 2 * GROUP
E_PITCH = 528
SPANS = [(0, 256), (256, 256), (512, 512), (1024, 512), (1536, 512)]
ACC_BANKS = 4


def tile_lag_channel_mix_s2_kernel(tc, x, e, a, c, w, v, bias, out):
    nc = tc.nc
    with ExitStack() as ctx:
        keep = ctx.enter_context(tc.tile_pool(name="keep", bufs=1))
        psum = ctx.enter_context(tc.psum_pool(name="psum", bufs=1))
        ctx.enter_context(tc.manual_schedule())

        ident = keep.tile([P, P], F32, name="ident")
        hist = keep.tile([P, C], BF16, name="hist")
        a_sb = keep.tile([P, 2, PACK], BF16, name="a_sb")
        c_sb = keep.tile([P, PACK], BF16, name="c_sb")
        bias_sb = keep.tile([P, N // P], BF16, name="bias_sb")
        bias_all = keep.tile([P, N], BF16, name="bias_all")
        x_words = [keep.tile([P, T], F32, name="x_words%d" % q) for q in range(4)]
        e_sb = [keep.tile([P, PACK, E_PITCH], BF16, name="e_sb%d" % i) for i in range(T // E_CHUNK)]
        w_codes, w_scales = {}, {}
        for g in range(3):
            for h in range(2):
                w_codes[g, h] = keep.tile([P, HALF], U32, name="w_codes%d%d" % (g, h), align_bytes=64)
                w_scales[g, h] = keep.tile([P, HALF], U8, name="w_scales%d%d" % (g, h), align_bytes=64)
        m_codes = [keep.tile([P, 2 * GROUP], U32, name="m_codes%d" % i, align_bytes=64) for i in range(GROUPS)]
        m_scales = [keep.tile([P, 2 * GROUP], U8, name="m_scales%d" % i, align_bytes=64) for i in range(GROUPS)]
        r_codes = [keep.tile([P, GROUP], U32, name="r_codes%d" % i, align_bytes=64) for i in range(GROUPS)]
        r_scales = [keep.tile([P, GROUP], U8, name="r_scales%d" % i, align_bytes=64) for i in range(GROUPS)]
        x_sb, w_rows, w_woven, x_bank, m_rows, m_woven = {}, {}, {}, {}, {}, {}
        scaled_e, r_rows, r_woven, acc = {}, {}, {}, {}

        def load_x(i):
            x_sb[i] = keep.tile([P, 2, C], BF16, name="x_sb", bufs=6)
            rows = x[LAG + GROUP * i : LAG + GROUP * (i + 1), :]
            nc.sync.dma_start(out=x_sb[i][:], in_=rows.rearrange("(s p) c -> p s c", p=P))

        def load_e(i):
            src = e.rearrange("(p j) t -> p j t", j=PACK)
            nc.sync.dma_start(out=e_sb[i][:, :, 0 : E_CHUNK + 1], in_=src[:, :, E_CHUNK * i : E_CHUNK * (i + 1) + 1])

        def load_w(g, h):
            w_rows[g, h] = keep.tile([P, PACK, HALF], BF16, name="w_rows", tag="w_rows%d%d" % (g, h), bufs=1, align_bytes=64)
            rows = w[K_PASS * g : K_PASS * (g + 1), :] if g < 2 else v
            src = rows.rearrange("(p j) n -> p j n", j=PACK)
            nc.sync.dma_start(out=w_rows[g, h][:], in_=src[:, :, HALF * h : HALF * (h + 1)])

        def weave(copy, dst, src):
            copy(out=dst.rearrange("p (c i j) -> p c j i", i=4, j=PACK), in_=src.rearrange("p j (c i) -> p c j i", i=4))

        def spread_bias():
            bank = psum.tile([P, 4, P], F32, name="bias_bank", tag="acc", bufs=ACC_BANKS)
            words = bias_sb[:].bitcast(F32)
            for j in range(4):
                nc.tensor.transpose(bank[:, j, :], words[:, j : j + 1].to_broadcast([P, P]), ident[:])
            dst = bias_all[:].bitcast(F32).rearrange("p (n j) -> p n j", j=4)
            nc.scalar.copy(out=dst, in_=bank[:].rearrange("p j n -> p n j"))

        def every_second_word(rows, q):
            g, u = divmod(q, 2)
            words_a_pass = K_PASS // 2
            return rows.bitcast(F32)[:, words_a_pass * g + u : words_a_pass * (g + 1) : 2]

        def turn_history():
            bank = psum.tile([P, 4, P], F32, name="hist_bank", tag="acc", bufs=ACC_BANKS)
            for q in range(4):
                nc.tensor.transpose(bank[:, q, :], every_second_word(hist[:], q), ident[:])
            for q in range(4):
                nc.scalar.copy(out=x_words[q][:, 0:LAG], in_=bank[:, q, 0:LAG])

        def turn_x(span):
            first, size = SPANS[span]
            for q in range(4):
                x_bank[span, q] = psum.tile([P, size], F32, name="x_bank%d" % q)
                for t in range(0, size, P):
                    i, s = divmod((first + t) // P, 2)
                    nc.tensor.transpose(x_bank[span, q][:, t : t + P], every_second_word(x_sb[i][:, s, :], q), ident[:])

        def keep_x(span):
            first, size = SPANS[span]
            count = min(size, T - LAG - first)
            for q in range(4):
                nc.scalar.copy(out=x_words[q][:, LAG + first : LAG + first + count], in_=x_bank[span, q][:, 0:count])

        def mix_m(span, q):
            first, size = SPANS[span]
            g, u = divmod(q, 2)
            if u == 0:
                m_rows[span, g] = keep.tile([P, PACK, size], BF16, name="m_rows", bufs=4)
            past = x_words[q][:].bitcast(BF16).rearrange("p (t d) -> p d t", d=2)
            now = x_bank[span, q][:].bitcast(BF16).rearrange("p (t d) -> p d t", d=2)
            for d in range(2):
                j = 2 * u + d
                nc.vector.scalar_tensor_tensor(
                    out=m_rows[span, g][:, j, :], in0=past[:, d, first : first + size], scalar=a_sb[:, g, j : j + 1],
                    in1=now[:, d, :], op0=MULT, op1=ADD)

        def weave_m(i, g):
            span = max(s for s in range(len(SPANS)) if SPANS[s][0] <= GROUP * i)
            off = GROUP * i - SPANS[span][0]
            if g == 0:
                m_woven[i] = keep.tile([P, 2, PACK * GROUP], BF16, name="m_woven", align_bytes=64, bufs=2)
            weave(nc.scalar.copy, m_woven[i][:, g, :], m_rows[span, g][:, :, off : off + GROUP])

        def quantize_m(i):
            nc.vector.quantize_mx(out=m_codes[i][:].bitcast(E4M3), scales=m_scales[i][:],
                                  in_=m_woven[i][:].rearrange("p g k -> p (g k)"))

        def mix_r_on_vector(chunk):
            rows = keep.tile([P, PACK, E_CHUNK], BF16, name="chunk_r_rows")
            for j in range(PACK):
                nc.vector.scalar_tensor_tensor(
                    out=rows[:, j, :], in0=e_sb[chunk][:, j, 0:E_CHUNK], scalar=c_sb[:, j : j + 1],
                    in1=e_sb[chunk][:, j, 1 : E_CHUNK + 1], op0=MULT, op1=ADD)
            for n in range(2):
                r_rows[2 * chunk + n] = rows[:, :, GROUP * n : GROUP * (n + 1)]

        def scale_e(i):
            scaled_e[i] = keep.tile([P, PACK, GROUP], F32, name="scaled_e", bufs=2)
            off = GROUP * (i % 2)
            for j in range(PACK):
                nc.gpsimd.tensor_scalar(out=scaled_e[i][:, j, :], in0=e_sb[i // 2][:, j, off : off + GROUP],
                                        scalar1=c_sb[:, j : j + 1], scalar2=0.0, op0=MULT, op1=ADD)

        def add_r(i, tag):
            rows = keep.tile([P, PACK, GROUP], BF16, name="r_rows", tag=tag, bufs=1, align_bytes=64)
            off = GROUP * (i % 2) + 1
            nc.gpsimd.tensor_tensor(out=rows[:], in0=e_sb[i // 2][:, :, off : off + GROUP], in1=scaled_e[i][:], op=ADD)
            r_rows[i] = rows[:]

        def weave_r(i):
            r_woven[i] = keep.tile([P, PACK * GROUP], BF16, name="r_woven", tag="r_woven%d" % i, bufs=1, align_bytes=64)
            weave(nc.scalar.copy, r_woven[i][:], r_rows[i])

        def quantize_r(i):
            nc.vector.quantize_mx(out=r_codes[i][:].bitcast(E5M2), scales=r_scales[i][:], in_=r_woven[i][:])

        def weave_w(g, h, copy):
            w_woven[g, h] = keep.tile([P, PACK * HALF], BF16, name="w_woven", tag="w_woven%d%d" % (g, h), bufs=1, align_bytes=64)
            weave(copy, w_woven[g, h][:], w_rows[g, h][:])

        def weave_on_gpsimd(src, tag):
            dst = keep.tile([P, PACK * src.shape[2]], BF16, name="woven", tag=tag, bufs=1, align_bytes=64)
            nc.gpsimd.tensor_scalar(out=dst[:].rearrange("p (n j) -> p n j", j=PACK), in0=src.rearrange("p j n -> p n j"),
                                    scalar1=1.0, scalar2=0.0, op0=MULT, op1=ADD)
            return dst

        def quantize_w(g, h):
            nc.vector.quantize_mx(out=w_codes[g, h][:].bitcast(E4M3), scales=w_scales[g, h][:], in_=w_woven[g, h][:])

        blocks = [(i, s, h) for h in range(2) for i in range(2) for s in range(2)]
        blocks = blocks + [(i, s, h) for i in range(2, GROUPS) for h in range(2) for s in range(2)]

        def multiply(k):
            i, s, h = blocks[k]
            acc[k] = psum.tile([P, HALF], F32, name="acc", tag="acc", bufs=ACC_BANKS)
            for g in range(2):
                cols = slice(GROUP * g + P * s, GROUP * g + P * (s + 1))
                nc.tensor.matmul_mx(out=acc[k][:], lhsT=m_codes[i][:, cols].bitcast(E4M3), lhsT_scale=m_scales[i][:, cols],
                                    rhs=w_codes[g, h][:].bitcast(E4M3), rhs_scale=w_scales[g, h][:],
                                    start=(g == 0), stop=False)
            cols = slice(P * s, P * (s + 1))
            nc.tensor.matmul_mx(out=acc[k][:], lhsT=r_codes[i][:, cols].bitcast(E5M2), lhsT_scale=r_scales[i][:, cols],
                                rhs=w_codes[2, h][:].bitcast(E4M3), rhs_scale=w_scales[2, h][:],
                                start=False, stop=True)

        def finish(k):
            i, s, h = blocks[k]
            row = GROUP * i + P * s
            width = HALF // 2 if k == len(blocks) - 1 else HALF
            for n in range(0, HALF, width):
                cols = slice(HALF * h + n, HALF * h + n + width)
                y = keep.tile([P, width], F32, name="y", bufs=12)
                nc.vector.tensor_tensor(out=y[:], in0=acc[k][:, n : n + width], in1=bias_all[:, cols], op=ADD)
                nc.sync.dma_start(out=out[row : row + P, cols], in_=y[:])

        def finish_and_refill(k, quantized):
            finish(k)
            later = k + ACC_BANKS
            if later < len(blocks) and blocks[later][0] < quantized:
                multiply(later)

        def weave_group(i):
            weave_m(i, 0)
            weave_m(i, 1)
            weave_r(i)

        def quantize_group(i):
            quantize_m(i)
            quantize_r(i)

        nc.vector.memset(hist[:], 0.0)
        make_identity(nc, ident[:])
        nc.scalar.dma_start(out=a_sb[:], in_=a.rearrange("(g p j) -> p g j", g=2, j=PACK))
        nc.scalar.dma_start(out=bias_sb[:], in_=bias.rearrange("(p j) -> p j", p=P))
        nc.scalar.dma_start(out=c_sb[:], in_=c.rearrange("(p j) -> p j", j=PACK))
        nc.scalar.dma_start(out=hist[0:LAG, :], in_=x[0:LAG, :])
        load_e(0)
        load_x(0)
        load_w(0, 0)
        load_w(1, 0)
        load_x(1)
        load_w(2, 0)
        load_x(2)
        load_x(3)
        load_w(0, 1)
        load_w(2, 1)
        load_w(1, 1)
        load_e(1)
        load_e(2)
        load_x(4)
        load_x(5)
        load_e(3)

        spread_bias()
        turn_history()
        mix_r_on_vector(0)
        weave_r(0)
        turn_x(0)
        keep_x(0)
        weave_r(1)
        weave_w(0, 0, nc.vector.tensor_copy)
        w_woven[1, 0] = weave_on_gpsimd(w_rows[1, 0][:], "w_rows00")
        w_woven[2, 0] = weave_on_gpsimd(w_rows[2, 0][:], "w_woven20")
        for q in range(4):
            mix_m(0, q)
        turn_x(1)
        load_x(6)
        load_x(7)
        keep_x(1)
        for q in range(4):
            mix_m(1, q)
        turn_x(2)
        weave_m(0, 0)
        weave_m(0, 1)
        quantize_w(0, 0)
        quantize_r(0)
        quantize_m(0)
        quantize_w(1, 0)
        quantize_w(2, 0)

        keep_x(2)
        multiply(0)
        multiply(1)
        w_woven[2, 1] = weave_on_gpsimd(w_rows[2, 1][:], "w_woven20")
        scale_e(4)
        weave_w(0, 1, nc.scalar.copy)
        weave_m(1, 0)
        weave_m(1, 1)
        weave_w(1, 1, nc.scalar.copy)
        mix_m(2, 0)
        mix_m(2, 1)
        finish(0)
        mix_m(2, 2)
        finish(1)
        mix_m(2, 3)
        turn_x(3)
        quantize_w(0, 1)
        mix_r_on_vector(1)
        quantize_group(1)
        quantize_w(2, 1)
        quantize_w(1, 1)

        keep_x(3)
        for k in range(2, 2 + ACC_BANKS):
            multiply(k)
        r_woven[2] = weave_on_gpsimd(r_rows[2], "w_woven11")
        add_r(4, "w_rows20")
        scale_e(5)
        weave_m(2, 0)
        weave_m(2, 1)
        weave_group(3)
        mix_m(3, 0)
        mix_m(3, 1)
        finish_and_refill(2, 2)
        mix_m(3, 2)
        finish_and_refill(3, 2)
        mix_m(3, 3)
        finish(4)
        finish(5)
        turn_x(4)
        keep_x(4)
        quantize_group(2)
        multiply(4 + ACC_BANKS)
        multiply(5 + ACC_BANKS)
        quantize_group(3)

        def finished_before(i):
            if i == 3:
                return 6
            beside_last_add = 1 if i + 1 == GROUPS - 1 else 0
            return 4 * (i - 1) + beside_last_add

        last_span, first_of_group_2, first_of_group_4 = len(SPANS) - 1, 8, 16
        for i in range(4, GROUPS):
            if i + 1 < GROUPS:
                add_r(i + 1, "r_woven%d" % (i - 1))
            if i + 2 < GROUPS:
                scale_e(i + 2)
            weave_group(i)
            step = range(finished_before(i - 1), finished_before(i))
            for k in step:
                if first_of_group_2 <= k < first_of_group_4 and k % 2 == 0:
                    mix_m(last_span, (k - first_of_group_2) // 2)
                finish_and_refill(k, i)
            quantize_group(i)
            for k in step:
                if blocks[k + ACC_BANKS][0] == i:
                    multiply(k + ACC_BANKS)
        for k in range(finished_before(GROUPS - 1), len(blocks)):
            finish_and_refill(k, GROUPS)
